import numpy as np, ml_dtypes
CORES = [6,15,38,47]
N = 4
import mx_ref
BF = ml_dtypes.bfloat16
def gentries(a):
    return np.ascontiguousarray(a.reshape(8, 16, -1).transpose(0, 2, 1)).reshape(8, -1)
def gtable(e):
    e = np.asarray(e); return np.ascontiguousarray(e.reshape(8, -1, 16).transpose(0, 2, 1)).reshape(128, -1).astype(np.int32)
def gcols(t, e):
    v = np.concatenate([t.reshape(8, 16, -1, 4), np.zeros((8, 16, 1, 4), BF)], axis=2)
    return np.ascontiguousarray(np.stack([v[g][:, e[g]] for g in range(8)])).reshape(128, -1)
def gpick(z, e):
    return np.concatenate([z[16 * g:16 * g + 16][:, e[g]] for g in range(8)])
def pick(q, e):
    c = np.concatenate([q[0].reshape(128, -1, 4), np.zeros((128, 1, 4), np.uint8)], axis=1); s = np.concatenate([q[1], np.ones((16, 1), np.uint8)], axis=1)
    return (np.ascontiguousarray(c[:, e].reshape(128, -1)), np.ascontiguousarray(s[:, e]))
def join(*qs):
    return (np.concatenate([q[0] for q in qs], axis=1), np.concatenate([q[1] for q in qs], axis=1))
def put(q, e, v):
    c, s = q[0].reshape(128, -1, 4).copy(), q[1].copy(); c[:, e] = v[0].reshape(128, -1, 4); s[:, e] = v[1]
    return (c.reshape(128, -1), s)
def pk(c, s):
    return (np.ascontiguousarray(c), mx_ref.live(s))
def emit(q):
    return q[0], q[1]
def packed(v, rng):
    q = [mx_ref.quantize(np.ascontiguousarray(v[r])) for r in range(N)]
    return np.stack([a for a, b in q]), np.stack([mx_ref.plane(b, rng) for a, b in q])
def values_of_codes():
    e, c = np.zeros((128, 128, 4), np.float32), np.zeros((128, 2, 4), np.uint8)
    e[np.arange(128), np.arange(128), 0] = 1
    c[:127, :, 0] = np.arange(256).reshape(2, 128).T[:127]
    return mx_ref.matmul(mx_ref.quantize(e.reshape(128, 512).astype(BF)), (c.reshape(128, 8), np.full((16, 2), 127, np.uint8))).T.reshape(-1).astype(np.float64)
CODE_VALUE, SCALE_VALUE = values_of_codes(), 2.0 ** (np.arange(256) - 127.0)
def decode(q):
    return (CODE_VALUE[q[0]].reshape(16, 8, -1, 4) * SCALE_VALUE[q[1]][:, None, :, None] + 0.0).reshape(128, -1).astype(np.float32)
def f(rng, *shape):
    return mx_ref.flush((rng.standard_normal(shape, dtype=np.float32) * np.exp2(rng.integers(-2, 3, shape[:-1] + (1,)))).astype(BF))
def wide(rng, *shape, cols=0):
    v = rng.standard_normal(shape, dtype=np.float32) * np.exp2(rng.integers(-12, 13, shape)).astype(np.float32)
    if cols: v *= np.repeat(np.exp2(rng.integers(-cols, cols + 1, shape[:-2] + (1, shape[-1] // 4))) * (rng.random(shape[:-2] + (1, shape[-1] // 4)) > 0.0625), 4, axis=-1).astype(np.float32)
    return mx_ref.flush(v.astype(BF))
V, F, K, T = 448, 896, 112, 2
def big(v, k):
    v = v.astype(np.float32) * np.float32(k)
    v[np.abs(v) < np.float32(2.0 ** -16)] = 0
    return v.astype(BF)
def weights(rng, k=1.0, still=slice(0)):
    v = big(f(rng, N, 128, 2048), k).reshape(N, 128, 4, 128, 4)
    v[:, :, :, still] = 0
    c, s = packed(v.reshape(N, 128, 2048), rng)
    return {"wc": c, "ws": s}
def lists_of(rng):
    return rng.permuted(np.tile(np.arange(F) % V, (N, 8, 1)), axis=2)
def stored(e):
    return np.stack([gtable(e[r]) for r in range(N)])
def numbers_of(rng):
    return {"x": big(f(rng, N, 128, 4 * V), 1), "fv": stored(lists_of(rng)), "u": np.array(f(rng, N, 128, 512)), "wy": np.array(f(rng, N, 128, 512))}
def planted(rng):
    at = 16 * rng.permutation(8)[:T]
    still = np.concatenate([np.arange(p, p + 16) for p in at])
    d = numbers_of(rng)
    x = d["x"].reshape(N, 128, V, 4)
    x[:, still] = 0
    d["u"][:, :, :4 * T] = 0
    d["u"][:, at, 4 * np.arange(T)] = 1
    return {**d, **weights(rng, 1.0, still)}, x, at
def setup_inputs(rng):
    return {**numbers_of(rng), **weights(rng)}
def setup_inputs_ties(rng):
    d, x, at = planted(rng)
    o = rng.permutation(N)
    none = int(rng.integers(T))
    for i in range(N):
        zero = i < N // 2
        for t in range(T):
            v = np.full(V, 0.0 if zero else 1.0, np.float32)
            j = rng.permutation(V)
            v[j[:K // 4]] = 2
            if zero: v[j[K // 4:K // 2]] = -2
            if i == 0: v *= np.float32(2.0 ** -24)
            if i == 0 and t == none: v[:] = 0
            if i == N - 1: v *= np.float32(2.0 ** 26)
            x[o[i], at[t], :, 0] = v.astype(BF)
    d["u"][o[0], at, 4 * np.arange(T)] = 2.0 ** -30
    d["u"][o[N - 1], at, 4 * np.arange(T)] = 2.0 ** 30
    return {**d, "x": x.reshape(N, 128, 4 * V)}
def setup_inputs_near(rng):
    d, x, at = planted(rng)
    e = lists_of(rng)
    sign = (rng.permutation(N) % 2 * 2.0 - 1.0).astype(np.float32).astype(BF)
    for t in range(T):
        p = int(at[t])
        e[:, p // 16] = np.arange(F) // 2
        d["u"][:, p + 1, 4 * t] = 2.0 ** 12
        d["u"][:, p + 8:p + 11, 4 * t:4 * t + 4] = 1
        x[:, p, :, 0] = sign[:, None]
        for r in range(N):
            s = np.argsort(np.argsort(np.arange(V) + 16 * rng.random(V)))
            s = (s + int(rng.integers(1, V // 4))) % V
            v = (((s[:, None] >> np.arange(12)) & 1) * np.exp2(np.arange(12) - 23.0)).astype(np.float32).astype(BF)
            x[r, p + 8:p + 11] = v.reshape(V, 3, 4).transpose(1, 0, 2)
            j = rng.permutation(V)[:8]
            x[r, p + 1, j[:4], 0] = 2.0 ** 30
            x[r, p + 1, j[4:], 0] = -2.0 ** 30
    m = int(rng.integers(N))
    later = [int(p) for p in at[1:]]
    d["u"][m, :, :4] = 0
    for p in range(0, 128, 16):
        if p in later: continue
        d["u"][m, p, 0] = 1
        d["u"][m, p + 8:p + 16, 0] = 1
        v = rng.integers(8, 16, (16, V, 4)) * rng.choice([-1.0, 1.0], (16, V, 4))
        v[:8] *= 2.0 ** -3
        v[8:] *= 2.0 ** -27
        v[0, :, 0] = 1
        x[m, p:p + 16] = v.astype(np.float32).astype(BF)
    return {**d, "x": x.reshape(N, 128, 4 * V), "fv": stored(e)}
def setup_inputs_deep(rng):
    d = numbers_of(rng)
    e = lists_of(rng)
    line = 1.0 - 2.0 * rng.integers(0, 2, (128, 4))
    sign = np.tile((rng.permutation(N) % 2 * 2.0 - 1.0)[:, None], (1, V))
    m = int(rng.permutation(np.flatnonzero(sign[:, 0] > 0))[0])
    j, k = rng.permutation(V), rng.permutation(F)
    sign[m, j[K // 4:]] = -1
    e[m][:, k[:K // 2]] = rng.permuted(np.tile(j[:K // 4], (8, 2)), axis=1)
    e[m][:, k[K // 2:]] = rng.permuted(np.tile(j[K // 4:], (8, 2)), axis=1)
    d["u"][:, :, :4 * T] = (np.tile(line, (1, T)) * 2.0 ** 30).astype(np.float32).astype(BF)
    x = np.where(rng.random((N, 128, V, 4)) < 0.0625, 0.875, 1.0) * 2.0 ** 30
    x = x * line[:, None, :] * sign[:, None, :, None]
    return {**d, "x": x.astype(np.float32).astype(BF).reshape(N, 128, 4 * V), "fv": stored(e), **weights(rng, 2.0 ** -5)}
def setup_inputs_crowd(rng):
    d, x, at = planted(rng)
    e = np.zeros((N, 8, F), int)
    for r in range(N):
        odd = bin(r).count("1") % 2
        turn = int(rng.integers(T))
        to = rng.permuted(np.tile(np.arange(V), (8, 1)), axis=1)
        e[r] = to[:, np.arange(F) % V if odd else np.arange(F) // 2]
        for t in range(T):
            v = np.ones(V, np.float32)
            if odd:
                j = 2 * rng.permutation(V // 2)[:K // 2] + rng.integers(0, 2, K // 2)
                if t == turn: j = 8 * rng.permutation(V // 8)[:K // 2] + int(rng.integers(8))
                v[j] = 64 * (1 + 0.25 * rng.integers(0, 4, K // 2))
            else:
                j = rng.permutation(V // 2)[:K // 4]
                up = rng.permutation(K // 4) % 2
                v[j + V // 2 * up] = 1024 * (1 + 0.25 * rng.integers(0, 4, K // 4))
                v[j + V // 2 * (1 - up)] = 64 * (1 + 0.25 * rng.integers(0, 4, K // 4))
            p = int(at[t])
            x[r, p, to[p // 16], 0] = v.astype(BF)
    return {**d, "x": x.reshape(N, 128, 4 * V), "fv": stored(e)}
def setup_inputs_spread(rng):
    d = setup_inputs(rng)
    d["x"] = big(wide(rng, N, 128, 4 * V, cols=6), 1)
    return d
def check_inputs(d):
    b = []
    for k in ("x", "u", "wy"):
        v = np.abs(d[k].astype(np.float32))
        if not (np.isfinite(v).all() and ((v == 0) | (v >= 2.0 ** -30) & (v <= 2.0 ** 30)).all()): b.append("a value of " + k)
    e = [gentries(a) for a in d["fv"]]
    if any(((a < 0) | (a >= V)).any() for a in e): b.append("an entry of fv out of range")
    if any((np.sort(a, axis=1) != np.arange(F) // 2).any() for a in e): b.append("a variable that isn't exactly twice in a list of fv")
    good = True
    for r in range(N):
        try:
            w = decode(pk(d["wc"][r], d["ws"][r]))
            good = good and bool(np.isfinite(w).all() and (np.abs(w) <= 2.0 ** 31).all())
        except Exception:
            good = False
    if not good: b.append("a number that wc and ws hold")
    return b
def reference(x, fv, u, wy, wc, ws):
    now = [x[r] for r in range(N)]
    e = [gentries(fv[r]) for r in range(N)]
    qu = [mx_ref.quantize(np.ascontiguousarray(u[r])) for r in range(N)]
    qw = [pk(wc[r], ws[r]) for r in range(N)]
    fl = np.zeros((N, T, K), np.float32)
    for t in range(T):
        fired, sent = [], []
        for r in range(N):
            h = mx_ref.quantize(gcols(now[r], e[r]))
            s = mx_ref.matmul(qu[r], h)[t] + np.float32(0.0)
            o = np.argsort(-s, kind="stable")[:K]
            fired.append(o)
            sent.append(pick(h, o))
            fl[r, t] = o
        new = []
        for r in range(N):
            p = r ^ (1 << t)
            low = np.full((8, V), K)
            np.minimum.at(low, (np.arange(8)[:, None], e[r][:, fired[p]]), np.tile(np.arange(K), (8, 1)))
            v = []
            for b in range(4):
                z = mx_ref.matmul(pick(qw[r], np.arange(128 * b, 128 * b + 128)), sent[p]) * np.float32(0.03125)
                v.append(gpick(np.concatenate([z, np.zeros((128, 1), np.float32)], axis=1), low))
            v = np.stack(v, axis=2).reshape(128, -1)
            hit = np.repeat(np.repeat(low < K, 16, axis=0), 4, axis=1)
            a = now[r].astype(np.float32)
            new.append(np.where(hit, a * np.float32(0.5) + v * np.float32(0.5), a).astype(BF))
        now = new
    y = np.zeros((N, 128, V), np.float32)
    oc, osc = np.zeros((N, 128, 4 * V), np.uint8), np.zeros((N, 16, V), np.uint8)
    for r in range(N):
        q = mx_ref.quantize(np.ascontiguousarray(now[r]))
        y[r] = mx_ref.matmul(mx_ref.quantize(np.ascontiguousarray(wy[r])), q)
        oc[r], osc[r] = emit(q)
    return {"y": y, "oc": oc, "osc": osc, "fl": fl}

@@ -1,0 +1,507 @@
+from concourse.mybir import dt, AluOpType, AxisListType, ActivationFunctionType
+
+V, F, K, ROUNDS = 448, 896, 112, 2
+LOW = 512
+TILES = F // 128
+SHARE = 160
+SPLIT = (272, 288)
+CB, SC = 128 + F + 2, F // 2 + 2
+LIFT, DROP = 131072.0, 1048576.0
+X4, U8, BF, F32, I32, U16, F16 = "float8_e4m3fn_x4", "uint8", "bfloat16", "float32", "int32", "uint16", "float16"
+
+
+def _scratch():
+    s = {}
+    def add(dtype, cols, *names):
+        for n in names:
+            s[n] = ("sbuf", [128, cols], dtype)
+    add(BF, 4 * V, "xs", "xi")
+    add(I32, 56, "fvi")
+    add(BF, 512, "us", "wys")
+    add(U16, 224, "l4")
+    add(U16, 56, "l1")
+    add(X4, 128, "qu", "qwy", "ur0", "ur1")
+    add(U8, 128, "su", "swy", "sr0", "sr1")
+    add(U16, 16, "oz", "lst0", "lst1")
+    add(X4, 512, "wq")
+    add(U8, 512, "wsc")
+    add(F32, F, "cnt", "fv256")
+    add(F32, K, "idb", "ids", "wa", "wb", "wm", "krow", "ks", "frow0", "frow1")
+    add(I32, K, "wi", "wj")
+    add(BF, 128, "ones", "hole")
+    add(I32, 16, "ci")
+    add(F32, 16, "cf")
+    add(U16, 2, "off16")
+    add(F32, 8, "kc", "kb", "neg0", "neg1", "acc", "ae", "al", "rk", "q1", "q2", "q3", "nth", "v256", "mm", "t1", "t2")
+    add(U16, 8, "ru", "got0", "got1", "ol0", "ol1")
+    add(U16, 28, "g40", "g41")
+    add(BF, 4 * F, "h0", "h1")
+    add(X4, F, "qh0", "qh1")
+    add(U8, F, "sh0", "sh1")
+    add(BF, TILES * CB, "cb")
+    add(F16, TILES * SC, "sc")
+    add(BF, F, "eq")
+    add(BF, TILES * LOW, "sg")
+    add(F32, 16 + F, "win0", "win1")
+    add(F32, 256, "tt")
+    add(X4, K, "slot0", "slot1")
+    add(U8, K, "sls0", "sls1")
+    add(X4, K + 128, "land0", "land1")
+    add(U8, K + 128, "lands0", "lands1")
+    add(F32, 4 * K, "ab", "x32")
+    add(BF, 4 * K, "n64")
+    add(BF, 2 * V, "pl0", "pl1", "pl2", "pl3")
+    add(X4, V, "qx")
+    add(U8, V, "sx")
+    add(F32, V, "ysb")
+    s["ps"] = ("psum", [128, 4096], F32)
+    return s
+
+
+SCRATCH = _scratch()
+POOL = {"v": 56, "s": 40, "t": 14, "g": 8}
+DMAS = 20
+SEMAPHORES = ([q + str(i) for q in POOL for i in range(POOL[q])] + ["d%d" % i for i in range(DMAS)]
+              + ["a%d" % i for i in range(3 * ROUNDS)] + ["sent"])
+
+
+def _meet(a, b):
+    if a[0] != b[0]:
+        return False
+    if a[0] == "ps":
+        return a[3] // 512 <= (b[4] - 1) // 512 and b[3] // 512 <= (a[4] - 1) // 512
+    if a[1] >= b[2] or b[1] >= a[2] or a[3] >= b[4] or b[3] >= a[4]:
+        return False
+    if a[5] == b[5]:
+        return (a[3] - b[3]) % a[5] == 0
+    if a[5] == 1:
+        a, b = b, a
+    if b[5] == 1:
+        return (a[3] - b[3]) % a[5] < b[4] - b[3]
+    return True
+
+
+def _emit(g, T, ops):
+    queue = {"v": g.vector, "s": g.scalar, "t": g.tensor, "g": g, "y": g.sync}
+    known = {q: 0 for q in queue}
+    seen, waits, needed = [], [], set()
+    for i, o in enumerate(ops):
+        q, deps = o["q"], []
+        if q != "far":
+            for j in range(i - 1, -1, -1):
+                e = ops[j]
+                hit = any(_meet(a, b) for a in o["r"] + o["w"] for b in e["w"]) or any(_meet(a, b) for a in o["w"] for b in e["r"])
+                if not hit and e["q"] != q:
+                    hit = any(a[0] == "ps" and _meet(a, b) for a in o["r"] for b in e["r"])
+                if hit and not known[q] >> j & 1:
+                    deps.append(j)
+                    needed.add(j)
+                    known[q] |= seen[j] | 1 << j
+        waits.append(deps)
+        seen.append(known[q] if q != "far" else 0)
+    last = {q: [[-1, 0] for k in range(POOL[q])] for q in POOL}
+    mark, total, dmas = {}, {}, [0]
+    for i, o in enumerate(ops):
+        q = o["q"]
+        if q == "far":
+            mark[i] = (o["sem"], o["n"])
+            total[o["sem"]] = o["n"]
+            continue
+        for j in reversed(waits[i]):
+            queue[q].wait_ge(T.sem[mark[j][0]], mark[j][1])
+        call = o["f"]()
+        if o["kind"] == "dma":
+            name = "d%d" % dmas[0]
+            dmas[0] += 1
+            call.then_inc(T.sem[name], 16)
+            mark[i] = (name, 16)
+            total[name] = 16
+        elif o["kind"] == "remote":
+            total["sent"] = total.get("sent", 0) + o["n"]
+        elif i in needed:
+            free = [k for k in range(POOL[q]) if last[q][k][0] < 0 or seen[i] >> last[q][k][0] & 1]
+            k = min(free or range(POOL[q]), key=lambda z: last[q][z][0])
+            last[q][k] = [i, last[q][k][1] + 1]
+            name = q + str(k)
+            call.then_inc(T.sem[name], 1)
+            mark[i] = (name, last[q][k][1])
+            total[name] = last[q][k][1]
+    waited = {}
+    for i, o in enumerate(ops):
+        for j in waits[i]:
+            waited[mark[j][0]] = max(waited.get(mark[j][0], 0), mark[j][1])
+    for name in sorted(total, key=lambda z: z[0] == "d"):
+        if waited.get(name, 0) < total[name]:
+            g.wait_ge(T.sem[name], total[name])
+
+
+def rank_program(g, core, T, topo):
+    rank = T.rank_of(core)
+    if rank is None:
+        return
+    A, ACT = AluOpType, ActivationFunctionType
+    ops = []
+
+    def R(name, c0=0, c1=None, step=1, p0=0, p1=128):
+        if c1 is None:
+            c1 = SCRATCH[name][1][1]
+        return (name, p0, p1, c0, c1 - (c1 - c0 - 1) % step, step)
+
+    def ap(r):
+        if not isinstance(r, tuple):
+            return r
+        if len(r) == 2:
+            return ap(r[0]).indirect(ap(r[1]))
+        rows = slice(None) if (r[1], r[2]) == (0, 128) else slice(r[1], r[2])
+        return T[r[0]][rows, r[3]:r[4]:r[5]] if r[5] > 1 else T[r[0]][rows, r[3]:r[4]]
+
+    def op(q, f, reads, writes, kind="op", n=0):
+        rd, wr = [], []
+        for r in reads:
+            if isinstance(r, tuple):
+                rd += list(r) if len(r) == 2 else [r]
+        for w in writes:
+            if len(w) == 2:
+                wr.append(w[0])
+                rd.append(w[1])
+            else:
+                wr.append(w)
+        ops.append({"q": q, "f": f, "r": rd, "w": wr, "kind": kind, "n": n})
+
+    def copy(out, in_):
+        op("v", lambda: g.vector.tensor_copy(ap(out), ap(in_)), [in_], [out])
+
+    def ts(out, in0, s1, op0, s2=None, op1=None):
+        if op1 is None:
+            op("v", lambda: g.vector.tensor_scalar(ap(out), ap(in0), ap(s1), None, op0), [in0, s1], [out])
+        else:
+            op("v", lambda: g.vector.tensor_scalar(ap(out), ap(in0), ap(s1), ap(s2), op0, op1), [in0, s1, s2], [out])
+
+    def tt(out, in0, in1, o):
+        op("v", lambda: g.vector.tensor_tensor(ap(out), ap(in0), ap(in1), o), [in0, in1], [out])
+
+    def scan(out, d0, d1, init, op0, op1):
+        op("v", lambda: g.vector.tensor_tensor_scan(ap(out), ap(d0), ap(d1), init, op0, op1), [d0, d1], [out])
+
+    def fill(out, c):
+        op("v", lambda: g.vector.memset(ap(out), c), [], [out])
+
+    def turn(out, in_):
+        op("v", lambda: g.vector.transpose(ap(out), ap(in_)), [in_], [out])
+
+    def act(out, in_, func, bias=0.0, scale=1.0, accum=None):
+        kw = {}
+        if isinstance(bias, tuple) or bias != 0.0:
+            kw["bias"] = bias
+        if scale != 1.0:
+            kw["scale"] = scale
+        if accum is not None:
+            kw["accum_out"] = accum
+        op("s", lambda: g.scalar.activation(ap(out), ap(in_), func, **{k: ap(kw[k]) for k in kw}),
+           [in_, bias], [out] + ([accum] if accum is not None else []))
+
+    def scaled(q, out, in_, c):
+        if q == "s":
+            act(out, in_, ACT.Copy, scale=c)
+        elif c == 1.0:
+            copy(out, in_)
+        else:
+            ts(out, in_, c, A.mult)
+
+    def quant(q, s, in_):
+        op("v", lambda: g.vector.quantize_mx(ap(q), ap(s), ap(in_)), [in_], [q, s])
+
+    def mx(bank, n, lq, ls, rq, rs):
+        out = R("ps", 512 * bank, 512 * bank + n)
+        op("t", lambda: g.tensor.matmul_mx(ap(out), ap(lq), ap(ls), ap(rq), ap(rs), True, True), [lq, ls, rq, rs], [out])
+
+    def pick_codes(out, win, off):
+        op("v", lambda: g.vector.tensor_copy(ap(out).bitcast(dt.uint32), ap(win).bitcast(dt.uint32).indirect(ap(off))), [win, off], [out])
+
+    def iota(out, pattern, base, mult, exact=True):
+        if exact:
+            op("g", lambda: g.iota(ap(out), pattern, base, mult), [], [out])
+        else:
+            op("g", lambda: g.iota(ap(out), pattern, base, mult, allow_small_or_imprecise_dtypes=True), [], [out])
+
+    def dma(q, out, in_, reads, writes):
+        e = g.sync if q == "y" else g.scalar
+        op(q, lambda: e.dma_start(out(), in_()), reads, writes, kind="dma")
+
+    def load(q, name, src, after=(), codes=False):
+        r = R(name)
+        dma(q, (lambda: ap(r).bitcast(dt.uint8)) if codes else (lambda: ap(r)), lambda: src[:], list(after), [r])
+
+    def send(t, k, src, dst, codes=False):
+        peer = T.cores[rank ^ (1 << t)]
+        rid, pid = topo.addr(peer)[:2]
+        n = len(topo.engines(core, peer))
+        view = (lambda r: ap(r).bitcast(dt.uint8)) if codes else ap
+        sem = "a%d" % (3 * t + k)
+        op("g", lambda: g.remote_dma(view(dst), view(src), T.sem[sem], T.sem["sent"], pid, rid, topo.mask(core, peer)), [src], [], kind="remote", n=n)
+        ops.append({"q": "far", "r": [], "w": [dst], "sem": sem, "n": len(topo.engines(peer, core)), "kind": "far"})
+
+    def col(name, c):
+        return R(name, c, c + 1)
+
+    width = [LOW] * 5 + [F - SHARE, F - LOW]
+
+    load("y", "fvi", T.fv)
+    load("s", "us", T.u)
+    load("y", "xs", T.x)
+    iota(col("ci", 0), [[0, 1]], 0, 1)
+    iota(R("wi"), [[1, K]], 128, -1)
+    iota(R("idb"), [[128, TILES], [1, 16]], 0, 0, False)
+    fill(R("ones"), 1.0)
+    op("g", lambda: g.affine_select(ap(R("hole")), ap(R("ones")), [[-1, 128]], A.not_equal, 0.0, 0, 1), [R("ones")], [R("hole")])
+    iota(R("cnt"), [[1, F]], 0, 0, False)
+    fill(R("oz", 0, 8), 0)
+    fill(R("oz", 8, 16), 1)
+    p = col("ci", 0)
+    ts(col("ci", 1), p, 7, A.bitwise_and)
+    ts(col("ci", 3), p, 4, A.arith_shift_right, 1, A.bitwise_and)
+    ts(col("ci", 4), p, 112, A.bitwise_and)
+    ts(col("ci", 5), p, 15, A.bitwise_and)
+    for t in range(ROUNDS):
+        fill(R("win%d" % t, 0, 144), 0.0)
+    tt(col("ci", 6), col("ci", 1), col("ci", 3), A.add)
+    tt(col("ci", 9), col("ci", 1), col("ci", 3), A.subtract)
+    copy(R("cf", 0, 2), R("ci", 4, 6))
+    ts(R("wj"), R("wi"), 15, A.bitwise_and)
+    ts(col("ci", 8), col("ci", 6), 1, A.bitwise_and)
+    ts(col("cf", 2), col("cf", 1), 15.0, A.is_lt, LIFT, A.mult)
+    ts(R("wa"), R("wj"), 0.0, A.is_equal, -DROP, A.mult)
+    ts(col("ci", 10), col("ci", 8), 9.0, A.mult)
+    ts(R("wb"), R("wj"), 1.0, A.is_equal, LIFT, A.mult)
+    ts(col("cf", 3), col("cf", 2), 72.0, A.add)
+    tt(col("ci", 11), col("ci", 10), col("ci", 9), A.add)
+    ts(R("ids"), R("idb"), col("cf", 0), A.add)
+    fill(R("cb", 128 + LOW, 5 * CB, CB), 0.0)
+    fill(col("cb", 5 * CB + 128 + width[5]), 0.0)
+    fill(col("cb", 6 * CB + 128 + width[6]), 0.0)
+    ts(col("off16", 0), col("ci", 11), 0.5, A.mult, 7.0, A.min)
+    tt(R("wm"), R("wa"), R("wb"), A.add)
+    for b in range(4):
+        ts(R("l4", 56 * b, 56 * b + 56), R("fvi"), 4.0, A.mult, float(b), A.add)
+    quant(R("qu"), R("su"), R("us"))
+    copy(R("l1"), R("fvi"))
+    pick_codes(R("ur0"), R("qu"), R("oz", 0, 8))
+    act(R("sr0"), (R("su"), R("oz", 0, 8)), ACT.Copy)
+    act(R("sr1"), (R("su"), R("oz", 8, 16)), ACT.Copy)
+    load("y", "wq", T.wc, [R("xs")], True)
+    load("y", "wsc", T.ws)
+    load("y", "wys", T.wy)
+
+    def gather_h(t, q, b, c0, c1):
+        out = R("h%d" % t, 4 * c0 + b, 4 * c1, 4)
+        if t == 0:
+            scaled(q, out, (R("xs"), R("l4", 56 * b + c0 // 16, 56 * b + c1 // 16)), 1.0)
+        else:
+            scaled(q, out, (R("pl%d" % b, 0, V), R("l1", c0 // 16, c1 // 16)), 1.0 / 64)
+
+    def ranks(t):
+        h, qh, sh, ur, sr, neg = ("%s%d" % (n, t) for n in ("h", "qh", "sh", "ur", "sr", "neg"))
+        used = [128] * TILES
+
+        def row(bank, a, b):
+            mx(bank, b - a, R(ur), R(sr), R(qh, a, b), R(sh, a, b))
+
+        def column(bank, j):
+            mx(bank, 128, R(qh, 128 * j, 128 * j + 128), R(sh, 128 * j, 128 * j + 128), R(ur), R(sr))
+
+        def v_count(j, a, b):
+            edge = min(max(128 * j + 128, a), b)
+            for lo, hi, o in ((a, edge, A.is_ge), (edge, b, A.is_gt)):
+                if hi > lo:
+                    at = CB * j + used[j]
+                    ts(R("cb", at, at + hi - lo), R("ps", lo, hi), col(neg, j), A.add, 0.0, o)
+                    used[j] += hi - lo
+
+        def v_equal(j):
+            ts(R("eq", 128 * j, 128 * j + 128), R("ps", 128 * j, 128 * j + 128), col(neg, j), A.add, 0.0, A.is_equal)
+
+        def v_ties(j):
+            scan(R("cb", CB * j, CB * j + 128), R("hole"), R("eq", 128 * j, 128 * j + 128), 0.0, A.mult, A.subtract)
+
+        def v_sum(j, start):
+            at, w = CB * j + 127, width[j] // 2 + 1
+            scan(R("sc", SC * (j + 1) - w, SC * (j + 1)), R("cb", at, at + w), R("cb", at + w, at + 2 * w), float(start), A.add, A.add)
+
+        def s_sign(j, a, b):
+            act(R("sg", LOW * j, LOW * j + b - a), R("ps", a, b), ACT.Sign, bias=col(neg, j))
+
+        def s_count(j, a, b, sign, into, out=None):
+            r = R("sg", LOW * j + a, LOW * j + b)
+            act(out or r, r, ACT.Relu, scale=sign, accum=col(into, j))
+
+        high = F - LOW
+        quant(R(qh, LOW, F), R(sh, LOW, F), R(h, 4 * LOW, 4 * F))
+        for j in (4, 5, 6):
+            column(j - 2, j)
+        row(1, LOW, F)
+        cut = SPLIT[t] // 32 * 32
+        gather_h(t, "s", 0, 0, LOW)
+        gather_h(t, "v", 3, 0, LOW)
+        gather_h(t, "s", 1, 0, LOW)
+        gather_h(t, "v", 2, cut, LOW)
+        gather_h(t, "s", 2, 0, cut)
+        scaled("v", R(neg, 4, TILES), R("ps", 1024, 2560, 512), -1.0)
+        v_count(6, LOW, F)
+        quant(R(qh, 0, LOW), R(sh, 0, LOW), R(h, 0, 4 * LOW))
+        s_sign(4, LOW, F)
+        for j in range(4):
+            column(4 + j, j)
+        row(0, 0, LOW)
+        row(2, 0, LOW)
+        v_equal(6)
+        v_equal(5)
+        v_count(5, LOW, F)
+        ts(R("eq", 512, 640), R("sg", 4 * LOW, 4 * LOW + 128), 0.0, A.is_equal)
+        s_count(4, 128, high, 1.0, "al")
+        s_count(4, 0, 128, -1.0, "ae", R("sg", 4 * LOW + high, 5 * LOW))
+        scaled("s", R(neg, 0, 4), R("ps", 2048, 4096, 512), -1.0)
+        s_sign(0, LOW, F)
+        act(col("acc", 4), col("ae", 4), ACT.Identity, bias=col("al", 4), scale=-1.0)
+        s_count(0, 0, high, 1.0, "acc")
+        s_sign(6, 1024, 1024 + LOW)
+        s_sign(5, 1024, 1024 + SHARE)
+        s_sign(1, LOW, F)
+        s_count(6, 0, LOW, -1.0, "ae")
+        s_count(5, 0, SHARE, -1.0, "ae")
+        s_sign(2, LOW, F)
+        s_count(1, 0, high, 1.0, "acc")
+        act(R("acc", 5, 7), R("ae", 5, 7), ACT.Copy, scale=-1.0)
+        s_sign(3, LOW, F)
+        s_count(2, 0, high, 1.0, "acc")
+        s_count(3, 0, high, 1.0, "acc")
+        for j in (6, 5, 4):
+            v_ties(j)
+        v_sum(6, LOW)
+        v_count(4, 0, LOW)
+        v_count(5, SHARE, LOW)
+        for j in range(4):
+            v_equal(j)
+        v_sum(4, 128)
+        v_sum(5, SHARE)
+        for j in range(4):
+            v_ties(j)
+        for j in range(4):
+            v_count(j, 0, LOW)
+            if j:
+                v_sum(j - 1, 0)
+        v_sum(3, 0)
+        tt(R("rk", 0, TILES), R("sc", SC - 1, SC * TILES, SC), R("acc", 0, TILES), A.add)
+        copy(R("ru", 0, TILES), R("rk", 0, TILES))
+
+    def fired(t):
+        win, lst = "win%d" % t, "lst%d" % t
+        copy((R(win, 16, 16 + F), R("ru", 0, TILES)), R("ids"))
+        turn(R("tt", 0, 128), R(win, 16, 144))
+        turn(R("tt", 128, 256), R(win, 0, 128))
+        tt(R("q1"), R("tt", 0, 256, 32), R("tt", 16, 256, 32), A.add)
+        tt(R("q2", p1=64), R("q1", p1=64), R("q1", p0=64), A.add)
+        for a in range(4):
+            tt(R("q3", p0=32 * a, p1=32 * a + 32), R("q2", p1=32), R("q2", p0=32, p1=64), A.add)
+        copy(R(lst), (R("q3"), col("off16", 0)))
+        off = R(lst, 0, TILES)
+        send(t, 0, R(lst, 0, 8), R("got%d" % t))
+        pick_codes(R("slot%d" % t), R("qh%d" % t), off)
+        act(R("sls%d" % t), (R("sh%d" % t), off), ACT.Copy)
+        send(t, 1, R("slot%d" % t), R("land%d" % t, 0, K), True)
+        send(t, 2, R("sls%d" % t), R("lands%d" % t, 0, K))
+
+    def report(t):
+        row = R("frow%d" % t)
+        copy(row, (R("cnt"), R("lst%d" % t, 0, TILES)))
+        dma("y", lambda: T.fl[t:t + 1, :], lambda: ap(R(row[0], p1=1)), [row], [])
+
+    def update(t):
+        got, g4, off = R("got%d" % t, 0, TILES), "g4%d" % t, R("ol%d" % t, 0, TILES)
+        tt(R("krow"), (R("fv256"), got), R("cnt", 0, K), A.add)
+        for b in range(4):
+            ts(R(g4, TILES * b, TILES * b + TILES), got, 4.0, A.mult, float(b), A.add)
+            if b == 1:
+                scan(R("ks"), R("wm"), R("krow"), 0.0, A.add, A.max)
+        kept = R("ks", 15, K, 16)
+        ts(R("nth", 0, TILES), kept, -1.0, A.mult, col("cf", 3), A.add)
+        tt(R("v256", 0, TILES), kept, R("kc", 0, TILES), A.subtract)
+        at = [8 * c * (c + 1) for c in range(TILES + 1)]
+        for c in reversed(range(TILES)):
+            act(R("ab", at[c], at[c + 1]), R("krow", 0, 16 * c + 16), ACT.Abs, bias=col("nth", c))
+        for a in (0, 2):
+            act(R("x32", K * a, K * a + 2 * K), (R("h%d" % t), R(g4, TILES * a, TILES * a + 2 * TILES)), ACT.Copy, scale=32.0)
+        for c in reversed(range(TILES)):
+            src, out = R("ab", at[c], at[c + 1]), col("mm", c)
+            op("v", lambda src=src, out=out: g.vector.tensor_reduce(ap(out), ap(src), AxisListType.X, A.min), [src], [out])
+        ts(R("t1", 0, TILES), R("mm", 0, TILES), 72.0, A.is_lt, 256.0 * V, A.mult)
+        tt(R("t2", 0, TILES), R("t1", 0, TILES), R("v256", 0, TILES), A.add)
+        ts(off, R("t2", 0, TILES), 1.0 / 256, A.mult)
+        for b in range(4):
+            mx(2 + b, 128, R("wq", 128 * b, 128 * b + 128), R("wsc", 128 * b, 128 * b + 128), R("land%d" % t, 0, 128), R("lands%d" % t, 0, 128))
+
+        def summed(b):
+            tt(R("n64", K * b, K * b + K), R("ps", 512 * (2 + b), 512 * (2 + b) + K), R("x32", K * b, K * b + K), A.add)
+        summed(0)
+        summed(1)
+        for b in range(4):
+            copy((R("pl%d" % b), off), R("n64", K * b, K * b + K))
+            if b + 2 < 4:
+                summed(b + 2)
+
+    gather_h(0, "s", 0, LOW, F)
+    gather_h(0, "v", 2, LOW, F)
+    gather_h(0, "s", 1, LOW, F)
+    gather_h(0, "v", 3, LOW, F)
+    ranks(0)
+    fired(0)
+    act(R("fv256"), (R("cnt", 0, V), R("l1")), ACT.Copy, scale=256.0)
+    ts(R("kb", 0, TILES), R("cnt", 0, K, 16), col("cf", 1), A.add)
+    for t in range(ROUNDS):
+        quant(R("land%d" % t, K, K + 128), R("lands%d" % t, K, K + 128), R("xs", 0, 512))
+    ts(R("kc", 0, TILES), R("kb", 0, TILES), col("cf", 2), A.add)
+    for b in range(4):
+        scaled("v", R("pl%d" % b, 0, V), R("xs", b, 4 * V, 4), 64.0)
+    report(0)
+    pick_codes(R("ur1"), R("qu"), R("oz", 8, 16))
+    update(0)
+
+    gather_h(1, "s", 0, LOW, F)
+    gather_h(1, "s", 1, LOW, F)
+    gather_h(1, "s", 2, LOW, F)
+    gather_h(1, "v", 3, LOW, F)
+    ranks(1)
+    fired(1)
+    report(1)
+    quant(R("qwy"), R("swy"), R("wys"))
+    update(1)
+
+    n = V // 2
+    for b in range(3):
+        scaled("s", R("xi", b, 4 * V, 4), R("pl%d" % b, 0, V), 1.0 / 64)
+    for half in range(2):
+        a, b = n * half, n * half + n
+        scaled("v", R("xi", 4 * a + 3, 4 * b, 4), R("pl3", a, b), 1.0 / 64)
+    for half in range(2):
+        a, b = n * half, n * half + n
+        q, s = R("qx", a, b), R("sx", a, b)
+        quant(q, s, R("xi", 4 * a, 4 * b))
+        mx(half, n, R("qwy"), R("swy"), q, s)
+        dma("y", lambda a=a, b=b: T.oc[:, 4 * a:4 * b], lambda q=q: ap(q).bitcast(dt.uint8), [q], [])
+
+    def store_scales(q, k):
+        s = R("sx", p0=32 * k, p1=32 * k + 4)
+        dma(q, lambda: T.osc[4 * k:4 * k + 4, :], lambda: ap(s), [s], [])
+
+    def store_y(q, half):
+        s = R("ysb", n * half, n * half + n)
+        dma(q, lambda: T.y[:, n * half:n * half + n], lambda: ap(s), [s], [])
+
+    act(R("ysb", 0, n), R("ps", 0, n), ACT.Copy)
+    copy(R("ysb", n, V), R("ps", 512, 512 + n))
+    store_y("s", 0)
+    store_scales("y", 0)
+    store_scales("y", 2)
+    store_y("y", 1)
+    store_scales("s", 1)
+    store_scales("s", 3)
+    _emit(g, T, ops)

@@ -3,8 +3,9 @@ from concourse.mybir import dt, AluOpType, AxisListType, ActivationFunctionType
 V, F, K, ROUNDS = 448, 896, 112, 2
 LOW = 512
 TILES = F // 128
-SHARE = 160
-SPLIT = (272, 288)
+SHARE = 384
+SPLIT = (448, 320)
+SLOT = (6, 3, 4, 5, 0, 1, 2)
 CB, SC = 128 + F + 2, F // 2 + 2
 LIFT, DROP = 131072.0, 1048576.0
 X4, U8, BF, F32, I32, U16, F16 = "float8_e4m3fn_x4", "uint8", "bfloat16", "float32", "int32", "uint16", "float16"
@@ -26,13 +27,13 @@ def _scratch():
     add(X4, 512, "wq")
     add(U8, 512, "wsc")
     add(F32, F, "cnt", "fv256")
-    add(F32, K, "idb", "ids", "wa", "wb", "wm", "krow", "ks", "frow0", "frow1")
+    add(F32, K, "idb", "ids", "wa", "wb", "wm", "krow", "kup", "ks", "frow0", "frow1")
     add(I32, K, "wi", "wj")
     add(BF, 128, "ones", "hole")
     add(I32, 16, "ci")
     add(F32, 16, "cf")
     add(U16, 2, "off16")
-    add(F32, 8, "kc", "kb", "neg0", "neg1", "acc", "ae", "al", "rk", "q1", "q2", "q3", "nth", "v256", "mm", "t1", "t2")
+    add(F32, 8, "kc", "kb", "neg0", "neg1", "acc", "ae", "al", "rk", "q1", "q2", "q3", "v256", "mm", "t1", "t2")
     add(U16, 8, "ru", "got0", "got1", "ol0", "ol1")
     add(U16, 28, "g40", "g41")
     add(BF, 4 * F, "h0", "h1")
@@ -246,12 +247,14 @@ def rank_program(g, core, T, topo):
 
     width = [LOW] * 5 + [F - SHARE, F - LOW]
 
-    load("y", "fvi", T.fv)
-    load("s", "us", T.u)
+    load("s", "fvi", T.fv)
     load("y", "xs", T.x)
+    load("y", "us", T.u)
     iota(col("ci", 0), [[0, 1]], 0, 1)
     iota(R("wi"), [[1, K]], 128, -1)
-    iota(R("idb"), [[128, TILES], [1, 16]], 0, 0, False)
+    iota(R("idb", 0, 48), [[128, 3], [1, 16]], 512, 0, False)
+    iota(R("idb", 48, 96), [[128, 3], [1, 16]], 128, 0, False)
+    iota(R("idb", 96, K), [[1, 16]], 0, 0, False)
     fill(R("ones"), 1.0)
     op("g", lambda: g.affine_select(ap(R("hole")), ap(R("ones")), [[-1, 128]], A.not_equal, 0.0, 0, 1), [R("ones")], [R("hole")])
     iota(R("cnt"), [[1, F]], 0, 0, False)
@@ -283,11 +286,7 @@ def rank_program(g, core, T, topo):
     tt(R("wm"), R("wa"), R("wb"), A.add)
     for b in range(4):
         ts(R("l4", 56 * b, 56 * b + 56), R("fvi"), 4.0, A.mult, float(b), A.add)
-    quant(R("qu"), R("su"), R("us"))
     copy(R("l1"), R("fvi"))
-    pick_codes(R("ur0"), R("qu"), R("oz", 0, 8))
-    act(R("sr0"), (R("su"), R("oz", 0, 8)), ACT.Copy)
-    act(R("sr1"), (R("su"), R("oz", 8, 16)), ACT.Copy)
     load("y", "wq", T.wc, [R("xs")], True)
     load("y", "wsc", T.ws)
     load("y", "wys", T.wy)
@@ -309,75 +308,81 @@ def rank_program(g, core, T, topo):
         def column(bank, j):
             mx(bank, 128, R(qh, 128 * j, 128 * j + 128), R(sh, 128 * j, 128 * j + 128), R(ur), R(sr))
 
-        def v_count(j, a, b):
+        def v_count(j, a, b, shift=0):
             edge = min(max(128 * j + 128, a), b)
             for lo, hi, o in ((a, edge, A.is_ge), (edge, b, A.is_gt)):
                 if hi > lo:
                     at = CB * j + used[j]
-                    ts(R("cb", at, at + hi - lo), R("ps", lo, hi), col(neg, j), A.add, 0.0, o)
+                    ts(R("cb", at, at + hi - lo), R("ps", shift + lo, shift + hi), col(neg, j), A.add, 0.0, o)
                     used[j] += hi - lo
 
-        def v_equal(j):
-            ts(R("eq", 128 * j, 128 * j + 128), R("ps", 128 * j, 128 * j + 128), col(neg, j), A.add, 0.0, A.is_equal)
+        def v_equal(j, shift=0):
+            ts(R("eq", 128 * j, 128 * j + 128), R("ps", shift + 128 * j, shift + 128 * j + 128), col(neg, j), A.add, 0.0, A.is_equal)
 
         def v_ties(j):
             scan(R("cb", CB * j, CB * j + 128), R("hole"), R("eq", 128 * j, 128 * j + 128), 0.0, A.mult, A.subtract)
 
         def v_sum(j, start):
-            at, w = CB * j + 127, width[j] // 2 + 1
-            scan(R("sc", SC * (j + 1) - w, SC * (j + 1)), R("cb", at, at + w), R("cb", at + w, at + 2 * w), float(start), A.add, A.add)
+            at, w, end = CB * j + 127, width[j] // 2 + 1, SC * (SLOT[j] + 1)
+            scan(R("sc", end - w, end), R("cb", at, at + w), R("cb", at + w, at + 2 * w), float(start), A.add, A.add)
 
         def s_sign(j, a, b):
             act(R("sg", LOW * j, LOW * j + b - a), R("ps", a, b), ACT.Sign, bias=col(neg, j))
 
         def s_count(j, a, b, sign, into, out=None):
             r = R("sg", LOW * j + a, LOW * j + b)
-            act(out or r, r, ACT.Relu, scale=sign, accum=col(into, j))
+            act(out or r, r, ACT.Relu, scale=sign, accum=col(into, SLOT[j]))
 
-        high = F - LOW
+        high, mid = F - LOW, LOW // 2
         quant(R(qh, LOW, F), R(sh, LOW, F), R(h, 4 * LOW, 4 * F))
         for j in (4, 5, 6):
             column(j - 2, j)
         row(1, LOW, F)
-        cut = SPLIT[t] // 32 * 32
         gather_h(t, "s", 0, 0, LOW)
-        gather_h(t, "v", 3, 0, LOW)
+        gather_h(t, "v", 3, 0, SPLIT[t])
         gather_h(t, "s", 1, 0, LOW)
-        gather_h(t, "v", 2, cut, LOW)
-        gather_h(t, "s", 2, 0, cut)
         scaled("v", R(neg, 4, TILES), R("ps", 1024, 2560, 512), -1.0)
-        v_count(6, LOW, F)
-        quant(R(qh, 0, LOW), R(sh, 0, LOW), R(h, 0, 4 * LOW))
-        s_sign(4, LOW, F)
-        for j in range(4):
-            column(4 + j, j)
+        row(3, LOW, F)
+        gather_h(t, "v", 2, 0, mid)
+        gather_h(t, "s", 2, mid, LOW)
+        gather_h(t, "s", 3, SPLIT[t], LOW)
+        quant(R(qh, 0, mid), R(sh, 0, mid), R(h, 0, 4 * mid))
+        column(4, 0)
+        column(5, 1)
+        v_count(6, LOW, F, 1024)
+        quant(R(qh, mid, LOW), R(sh, mid, LOW), R(h, 4 * mid, 4 * LOW))
         row(0, 0, LOW)
+        column(6, 2)
+        column(7, 3)
         row(2, 0, LOW)
-        v_equal(6)
-        v_equal(5)
-        v_count(5, LOW, F)
-        ts(R("eq", 512, 640), R("sg", 4 * LOW, 4 * LOW + 128), 0.0, A.is_equal)
+        s_sign(4, LOW, F)
         s_count(4, 128, high, 1.0, "al")
         s_count(4, 0, 128, -1.0, "ae", R("sg", 4 * LOW + high, 5 * LOW))
-        scaled("s", R(neg, 0, 4), R("ps", 2048, 4096, 512), -1.0)
-        s_sign(0, LOW, F)
-        act(col("acc", 4), col("ae", 4), ACT.Identity, bias=col("al", 4), scale=-1.0)
-        s_count(0, 0, high, 1.0, "acc")
+        scaled("s", R(neg, 0, 2), R("ps", 2048, 3072, 512), -1.0)
+        s_sign(1, LOW, F)
+        act(col("acc", 0), col("ae", 0), ACT.Identity, bias=col("al", 0), scale=-1.0)
+        s_count(1, 0, high, 1.0, "acc")
+        scaled("s", R(neg, 2, 4), R("ps", 3072, 4096, 512), -1.0)
         s_sign(6, 1024, 1024 + LOW)
         s_sign(5, 1024, 1024 + SHARE)
-        s_sign(1, LOW, F)
+        s_sign(2, LOW, F)
         s_count(6, 0, LOW, -1.0, "ae")
         s_count(5, 0, SHARE, -1.0, "ae")
-        s_sign(2, LOW, F)
-        s_count(1, 0, high, 1.0, "acc")
-        act(R("acc", 5, 7), R("ae", 5, 7), ACT.Copy, scale=-1.0)
         s_sign(3, LOW, F)
+        act(R("acc", 1, 3), R("ae", 1, 3), ACT.Copy, scale=-1.0)
         s_count(2, 0, high, 1.0, "acc")
         s_count(3, 0, high, 1.0, "acc")
-        for j in (6, 5, 4):
-            v_ties(j)
-        v_sum(6, LOW)
+        s_sign(0, LOW, F)
+        s_count(0, 0, high, 1.0, "acc")
+        v_equal(6, 1024)
+        v_equal(5, 1024)
+        v_count(5, LOW, F, 1024)
+        ts(R("eq", 512, 640), R("sg", 4 * LOW, 4 * LOW + 128), 0.0, A.is_equal)
+        v_ties(6)
+        v_ties(5)
         v_count(4, 0, LOW)
+        v_ties(4)
+        v_sum(6, LOW)
         v_count(5, SHARE, LOW)
         for j in range(4):
             v_equal(j)
@@ -385,17 +390,24 @@ def rank_program(g, core, T, topo):
         v_sum(5, SHARE)
         for j in range(4):
             v_ties(j)
-        for j in range(4):
-            v_count(j, 0, LOW)
-            if j:
-                v_sum(j - 1, 0)
+        v_count(1, 0, LOW)
+        v_count(2, 0, LOW)
+        v_sum(1, 0)
+        v_count(3, 0, LOW)
+        v_sum(2, 0)
+        v_count(0, 0, 128)
         v_sum(3, 0)
-        tt(R("rk", 0, TILES), R("sc", SC - 1, SC * TILES, SC), R("acc", 0, TILES), A.add)
-        copy(R("ru", 0, TILES), R("rk", 0, TILES))
+        v_count(0, 128, LOW)
+        tt(R("rk", 0, 6), R("sc", SC - 1, SC * 6, SC), R("acc", 0, 6), A.add)
+        v_sum(0, 0)
+        copy(R("ru", 0, 6), R("rk", 0, 6))
+        win = R("win%d" % t, 16, 16 + F)
+        copy((win, R("ru", 0, 6)), R("ids", 0, 96))
+        ts(col("ru", 6), col("sc", SC * TILES - 1), col("acc", 6), A.add)
+        copy((win, col("ru", 6)), R("ids", 96, K))
 
     def fired(t):
         win, lst = "win%d" % t, "lst%d" % t
-        copy((R(win, 16, 16 + F), R("ru", 0, TILES)), R("ids"))
         turn(R("tt", 0, 128), R(win, 16, 144))
         turn(R("tt", 128, 256), R(win, 0, 128))
         tt(R("q1"), R("tt", 0, 256, 32), R("tt", 16, 256, 32), A.add)
@@ -421,48 +433,53 @@ def rank_program(g, core, T, topo):
         for b in range(4):
             ts(R(g4, TILES * b, TILES * b + TILES), got, 4.0, A.mult, float(b), A.add)
             if b == 1:
+                ts(R("kup"), R("krow"), col("cf", 3), A.add)
                 scan(R("ks"), R("wm"), R("krow"), 0.0, A.add, A.max)
-        kept = R("ks", 15, K, 16)
-        ts(R("nth", 0, TILES), kept, -1.0, A.mult, col("cf", 3), A.add)
-        tt(R("v256", 0, TILES), kept, R("kc", 0, TILES), A.subtract)
         at = [8 * c * (c + 1) for c in range(TILES + 1)]
-        for c in reversed(range(TILES)):
-            act(R("ab", at[c], at[c + 1]), R("krow", 0, 16 * c + 16), ACT.Abs, bias=col("nth", c))
+        ts(R("ab", 0, 16), R("kup", 0, 16), col("ks", 15), A.subtract)
+        tt(R("v256", 0, TILES), R("ks", 15, K, 16), R("kc", 0, TILES), A.subtract)
+        for c in range(TILES - 1, 0, -1):
+            act(R("ab", at[c], at[c + 1]), R("kup", 0, 16 * c + 16), ACT.Abs, bias=col("ks", 16 * c + 15), scale=-1.0)
         for a in (0, 2):
             act(R("x32", K * a, K * a + 2 * K), (R("h%d" % t), R(g4, TILES * a, TILES * a + 2 * TILES)), ACT.Copy, scale=32.0)
-        for c in reversed(range(TILES)):
+        for c in (0, 6, 5, 4, 3, 2, 1):
             src, out = R("ab", at[c], at[c + 1]), col("mm", c)
-            op("v", lambda src=src, out=out: g.vector.tensor_reduce(ap(out), ap(src), AxisListType.X, A.min), [src], [out])
-        ts(R("t1", 0, TILES), R("mm", 0, TILES), 72.0, A.is_lt, 256.0 * V, A.mult)
-        tt(R("t2", 0, TILES), R("t1", 0, TILES), R("v256", 0, TILES), A.add)
-        ts(off, R("t2", 0, TILES), 1.0 / 256, A.mult)
+            op("v", lambda src=src, out=out: g.vector.tensor_reduce(ap(out), ap(src), AxisListType.X, A.min, apply_absolute_value=True), [src], [out])
         for b in range(4):
             mx(2 + b, 128, R("wq", 128 * b, 128 * b + 128), R("wsc", 128 * b, 128 * b + 128), R("land%d" % t, 0, 128), R("lands%d" % t, 0, 128))
 
         def summed(b):
             tt(R("n64", K * b, K * b + K), R("ps", 512 * (2 + b), 512 * (2 + b) + K), R("x32", K * b, K * b + K), A.add)
+        ts(R("t1", 0, TILES), R("mm", 0, TILES), 72.0, A.is_lt, 256.0 * V, A.mult)
         summed(0)
+        tt(R("t2", 0, TILES), R("t1", 0, TILES), R("v256", 0, TILES), A.add)
         summed(1)
+        ts(off, R("t2", 0, TILES), 1.0 / 256, A.mult)
+        summed(2)
         for b in range(4):
             copy((R("pl%d" % b), off), R("n64", K * b, K * b + K))
-            if b + 2 < 4:
-                summed(b + 2)
+            if b == 0:
+                summed(3)
 
     gather_h(0, "s", 0, LOW, F)
     gather_h(0, "v", 2, LOW, F)
     gather_h(0, "s", 1, LOW, F)
-    gather_h(0, "v", 3, LOW, F)
+    quant(R("qu"), R("su"), R("us"))
+    gather_h(0, "v", 3, LOW, F - 96)
+    gather_h(0, "s", 3, F - 96, F)
+    pick_codes(R("ur0"), R("qu"), R("oz", 0, 8))
+    act(R("sr0"), (R("su"), R("oz", 0, 8)), ACT.Copy)
     ranks(0)
     fired(0)
-    act(R("fv256"), (R("cnt", 0, V), R("l1")), ACT.Copy, scale=256.0)
+    scaled("s", R("fv256", 0, 640), (R("cnt", 0, V), R("l1", 0, 40)), 256.0)
+    scaled("v", R("fv256", 640, F), (R("cnt", 0, V), R("l1", 40, 56)), 256.0)
     ts(R("kb", 0, TILES), R("cnt", 0, K, 16), col("cf", 1), A.add)
-    for t in range(ROUNDS):
-        quant(R("land%d" % t, K, K + 128), R("lands%d" % t, K, K + 128), R("xs", 0, 512))
+    quant(R("land0", K, K + 128), R("lands0", K, K + 128), R("xs", 0, 512))
     ts(R("kc", 0, TILES), R("kb", 0, TILES), col("cf", 2), A.add)
     for b in range(4):
-        scaled("v", R("pl%d" % b, 0, V), R("xs", b, 4 * V, 4), 64.0)
-    report(0)
+        scaled("vvvs"[b], R("pl%d" % b, 0, V), R("xs", b, 4 * V, 4), 64.0)
     pick_codes(R("ur1"), R("qu"), R("oz", 8, 16))
+    act(R("sr1"), (R("su"), R("oz", 8, 16)), ACT.Copy)
     update(0)
 
     gather_h(1, "s", 0, LOW, F)
@@ -471,6 +488,8 @@ def rank_program(g, core, T, topo):
     gather_h(1, "v", 3, LOW, F)
     ranks(1)
     fired(1)
+    quant(R("land1", K, K + 128), R("lands1", K, K + 128), R("xs", 0, 512))
+    report(0)
     report(1)
     quant(R("qwy"), R("swy"), R("wys"))
     update(1)
@@ -478,9 +497,8 @@ def rank_program(g, core, T, topo):
     n = V // 2
     for b in range(3):
         scaled("s", R("xi", b, 4 * V, 4), R("pl%d" % b, 0, V), 1.0 / 64)
-    for half in range(2):
-        a, b = n * half, n * half + n
-        scaled("v", R("xi", 4 * a + 3, 4 * b, 4), R("pl3", a, b), 1.0 / 64)
+    for a in (0, n):
+        scaled("v", R("xi", 4 * a + 3, 4 * (a + n), 4), R("pl3", a, a + n), 1.0 / 64)
     for half in range(2):
         a, b = n * half, n * half + n
         q, s = R("qx", a, b), R("sx", a, b)

@@ -1,14 +1,17 @@
-from concourse.mybir import dt, AluOpType, AxisListType, ActivationFunctionType
+from concourse.mybir import dt, AluOpType, ActivationFunctionType
 
 V, F, K, ROUNDS = 448, 896, 112, 2
-LOW = 512
 TILES = F // 128
-SHARE = 384
-SPLIT = (448, 320)
-SLOT = (6, 3, 4, 5, 0, 1, 2)
-CB, SC = 128 + F + 2, F // 2 + 2
-LIFT, DROP = 131072.0, 1048576.0
+CB, SC, SG = 128 + F + 2, 450, 768
+PL = 3 * V
 X4, U8, BF, F32, I32, U16, F16 = "float8_e4m3fn_x4", "uint8", "bfloat16", "float32", "int32", "uint16", "float16"
+P = {"parts": [(0, 384), (384, 640), (640, 896)],
+     "pivots": [[5, 6, 7], [6, 7], [6, 7]],
+     "scalar": [(384, 640), (640, 896), (640, 896), (640, 896), (640, 896), (0, 384), (0, 384)],
+     "runs": [(0, 4), (4, 7)],
+     "out": (224, 224)}
+QUEUES = "svvssvssvsvsssvvsssvvsssvsssvsssssvsvvssvvvsssssssssvv"
+ORDER = [0,1,5,37,22,2,3,36,4,30,34,9,11,14,12,163,33,13,31,35,32,6,15,8,24,26,17,25,16,164,23,38,18,27,42,45,10,28,7,29,39,44,43,67,40,19,46,41,69,68,48,165,47,66,49,20,93,51,90,52,70,50,92,168,21,71,60,72,61,75,91,65,74,56,57,73,94,62,76,58,83,80,99,53,96,77,88,98,103,95,81,63,79,105,59,101,54,97,64,82,104,100,106,78,85,115,84,107,55,125,109,124,102,126,86,114,116,108,110,130,123,112,87,89,133,134,117,119,131,121,111,113,132,127,118,128,122,120,135,136,129,137,138,139,140,141,142,143,169,144,145,148,153,170,147,154,166,171,158,172,155,167,157,161,149,151,146,174,175,156,160,176,159,181,183,178,184,177,180,179,189,182,150,186,185,152,192,190,187,195,193,191,198,162,196,188,194,200,197,201,228,204,199,202,205,203,206,254,227,207,230,251,213,229,253,209,210,208,252,212,231,211,255,233,218,232,214,226,236,223,234,235,217,237,260,215,222,241,257,221,246,224,256,219,264,244,259,266,240,258,262,216,242,247,270,239,265,225,220,243,238,261,277,282,263,285,249,267,280,286,271,248,284,273,245,291,275,268,278,287,274,293,272,279,276,292,269,295,294,250,281,283,289,296,288,297,290,299,298,300,301,302,303,304,173,305,306,309,308,322,316,315,310,314,312,307,327,326,323,328,318,325,333,332,334,335,329,336,330,341,331,317,311,338,337,313,347,339,344,342,348,340,345,343,350,349,351,352,346,356,357,353,355,354,319,358,320,321,324,359,364,360,361,365,370,366,362,371,367,363,368,372,369]
 
 
 def _scratch():
@@ -16,7 +19,8 @@ def _scratch():
     def add(dtype, cols, *names):
         for n in names:
             s[n] = ("sbuf", [128, cols], dtype)
-    add(BF, 4 * V, "xs", "xi")
+    add(BF, 4 * V, "xs")
+    add(BF, 4 * PL, "xi")
     add(I32, 56, "fvi")
     add(BF, 512, "us", "wys")
     add(U16, 224, "l4")
@@ -26,32 +30,32 @@ def _scratch():
     add(U16, 16, "oz", "lst0", "lst1")
     add(X4, 512, "wq")
     add(U8, 512, "wsc")
-    add(F32, F, "cnt", "fv256")
-    add(F32, K, "idb", "ids", "wa", "wb", "wm", "krow", "kup", "ks", "frow0", "frow1")
-    add(I32, K, "wi", "wj")
+    add(F32, F, "cnt", "fvt")
+    add(F32, K, "ids", "idb", "dm", "sm", "vrow", "vm", "own", "frev0", "frev1", "frow0", "frow1")
     add(BF, 128, "ones", "hole")
     add(I32, 16, "ci")
-    add(F32, 16, "cf")
+    add(I32, 8, "rvi")
+    add(F32, 8, "cf", "q1", "q2", "q3", "pos0", "pos1", "sa", "sb", "r1")
     add(U16, 2, "off16")
-    add(F32, 8, "kc", "kb", "neg0", "neg1", "acc", "ae", "al", "rk", "q1", "q2", "q3", "v256", "mm", "t1", "t2")
-    add(U16, 8, "ru", "got0", "got1", "ol0", "ol1")
-    add(U16, 28, "g40", "g41")
+    add(U16, 8, "ru", "got0", "got1", "ol0", "ow0", "ow1", "rev")
+    add(U16, 28, "ol1")
     add(BF, 4 * F, "h0", "h1")
     add(X4, F, "qh0", "qh1")
     add(U8, F, "sh0", "sh1")
-    add(BF, TILES * CB, "cb")
+    add(F16, TILES * CB, "cb")
     add(F16, TILES * SC, "sc")
-    add(BF, F, "eq")
-    add(BF, TILES * LOW, "sg")
+    add(BF, F, "eq", "rm")
+    add(F16, TILES * K, "ev", "dd")
+    add(BF, TILES * SG, "sg", "sg2")
     add(F32, 16 + F, "win0", "win1")
     add(F32, 256, "tt")
     add(X4, K, "slot0", "slot1")
     add(U8, K, "sls0", "sls1")
     add(X4, K + 128, "land0", "land1")
     add(U8, K + 128, "lands0", "lands1")
-    add(F32, 4 * K, "ab", "x32")
-    add(BF, 4 * K, "n64")
-    add(BF, 2 * V, "pl0", "pl1", "pl2", "pl3")
+    add(F32, 4 * K, "x32")
+    add(BF, 4 * K, "n64", "nx")
+    add(BF, PL, "pl0", "pl1", "pl2", "pl3")
     add(X4, V, "qx")
     add(U8, V, "sx")
     add(F32, V, "ysb")
@@ -60,7 +64,7 @@ def _scratch():
 
 
 SCRATCH = _scratch()
-POOL = {"v": 56, "s": 40, "t": 14, "g": 8}
+POOL = {"v": 56, "s": 40, "t": 14, "g": 12}
 DMAS = 20
 SEMAPHORES = ([q + str(i) for q in POOL for i in range(POOL[q])] + ["d%d" % i for i in range(DMAS)]
               + ["a%d" % i for i in range(3 * ROUNDS)] + ["sent"])
@@ -82,6 +86,26 @@ def _meet(a, b):
     return True
 
 
+def _hazard(o, e):
+    return any(_meet(a, b) for a in o["r"] + o["w"] for b in e["w"]) or any(_meet(a, b) for a in o["w"] for b in e["r"])
+
+
+def _units(ops):
+    units = []
+    for o in ops:
+        if o.get("glue") and units and units[-1][-1].get("glue") == o["glue"]:
+            units[-1].append(o)
+        else:
+            units.append([o])
+    return units
+
+
+def _order(ops):
+    units = _units(ops)
+    assert sorted(ORDER) == list(range(len(units)))
+    return [o for i in ORDER for o in units[i]]
+
+
 def _emit(g, T, ops):
     queue = {"v": g.vector, "s": g.scalar, "t": g.tensor, "g": g, "y": g.sync}
     known = {q: 0 for q in queue}
@@ -90,11 +114,13 @@ def _emit(g, T, ops):
         q, deps = o["q"], []
         if q != "far":
             for j in range(i - 1, -1, -1):
+                if known[q] >> j & 1:
+                    continue
                 e = ops[j]
-                hit = any(_meet(a, b) for a in o["r"] + o["w"] for b in e["w"]) or any(_meet(a, b) for a in o["w"] for b in e["r"])
+                hit = _hazard(o, e)
                 if not hit and e["q"] != q:
                     hit = any(a[0] == "ps" and _meet(a, b) for a in o["r"] for b in e["r"])
-                if hit and not known[q] >> j & 1:
+                if hit:
                     deps.append(j)
                     needed.add(j)
                     known[q] |= seen[j] | 1 << j
@@ -142,6 +168,7 @@ def rank_program(g, core, T, topo):
         return
     A, ACT = AluOpType, ActivationFunctionType
     ops = []
+    state = {"after": [], "glue": None, "copies": 0}
 
     def R(name, c0=0, c1=None, step=1, p0=0, p1=128):
         if c1 is None:
@@ -157,7 +184,7 @@ def rank_program(g, core, T, topo):
         return T[r[0]][rows, r[3]:r[4]:r[5]] if r[5] > 1 else T[r[0]][rows, r[3]:r[4]]
 
     def op(q, f, reads, writes, kind="op", n=0):
-        rd, wr = [], []
+        rd, wr = list(state["after"]), []
         for r in reads:
             if isinstance(r, tuple):
                 rd += list(r) if len(r) == 2 else [r]
@@ -167,7 +194,7 @@ def rank_program(g, core, T, topo):
                 rd.append(w[1])
             else:
                 wr.append(w)
-        ops.append({"q": q, "f": f, "r": rd, "w": wr, "kind": kind, "n": n})
+        ops.append({"q": q, "f": f, "r": rd, "w": wr, "kind": kind, "n": n, "glue": state["glue"]})
 
     def copy(out, in_):
         op("v", lambda: g.vector.tensor_copy(ap(out), ap(in_)), [in_], [out])
@@ -192,7 +219,7 @@ def rank_program(g, core, T, topo):
 
     def act(out, in_, func, bias=0.0, scale=1.0, accum=None):
         kw = {}
-        if isinstance(bias, tuple) or bias != 0.0:
+        if isinstance(bias, tuple):
             kw["bias"] = bias
         if scale != 1.0:
             kw["scale"] = scale
@@ -201,13 +228,16 @@ def rank_program(g, core, T, topo):
         op("s", lambda: g.scalar.activation(ap(out), ap(in_), func, **{k: ap(kw[k]) for k in kw}),
            [in_, bias], [out] + ([accum] if accum is not None else []))
 
-    def scaled(q, out, in_, c):
-        if q == "s":
+    def scaled(out, in_, c=1.0):
+        k = state["copies"]
+        state["copies"] = k + 1
+        if QUEUES[k] == "s":
             act(out, in_, ACT.Copy, scale=c)
         elif c == 1.0:
             copy(out, in_)
         else:
             ts(out, in_, c, A.mult)
+        ops[-1]["either"] = k
 
     def quant(q, s, in_):
         op("v", lambda: g.vector.quantize_mx(ap(q), ap(s), ap(in_)), [in_], [q, s])
@@ -245,281 +275,223 @@ def rank_program(g, core, T, topo):
     def col(name, c):
         return R(name, c, c + 1)
 
-    width = [LOW] * 5 + [F - SHARE, F - LOW]
-
     load("s", "fvi", T.fv)
     load("y", "xs", T.x)
     load("y", "us", T.u)
-    iota(col("ci", 0), [[0, 1]], 0, 1)
-    iota(R("wi"), [[1, K]], 128, -1)
-    iota(R("idb", 0, 48), [[128, 3], [1, 16]], 512, 0, False)
-    iota(R("idb", 48, 96), [[128, 3], [1, 16]], 128, 0, False)
-    iota(R("idb", 96, K), [[1, 16]], 0, 0, False)
-    fill(R("ones"), 1.0)
-    op("g", lambda: g.affine_select(ap(R("hole")), ap(R("ones")), [[-1, 128]], A.not_equal, 0.0, 0, 1), [R("ones")], [R("hole")])
+    p = col("ci", 0)
+    iota(p, [[0, 1]], 0, 1)
+    iota(R("idb"), [[128, TILES], [1, 16]], 0, 0, False)
+    iota(R("ones"), [[0, 128]], 1, 0, False)
+    op("g", lambda: g.affine_select(ap(R("hole")), ap(R("ones")), [[-1, 128]], A.not_equal, -1.0, 0, 1), [R("ones")], [R("hole")])
     iota(R("cnt"), [[1, F]], 0, 0, False)
     fill(R("oz", 0, 8), 0)
     fill(R("oz", 8, 16), 1)
-    p = col("ci", 0)
+    iota(R("win0", F - 128, F + 16), [[0, 144]], 0, 0, False)
     ts(col("ci", 1), p, 7, A.bitwise_and)
     ts(col("ci", 3), p, 4, A.arith_shift_right, 1, A.bitwise_and)
     ts(col("ci", 4), p, 112, A.bitwise_and)
     ts(col("ci", 5), p, 15, A.bitwise_and)
-    for t in range(ROUNDS):
-        fill(R("win%d" % t, 0, 144), 0.0)
+    copy(R("cf", 0, 2), R("ci", 4, 6))
     tt(col("ci", 6), col("ci", 1), col("ci", 3), A.add)
     tt(col("ci", 9), col("ci", 1), col("ci", 3), A.subtract)
-    copy(R("cf", 0, 2), R("ci", 4, 6))
-    ts(R("wj"), R("wi"), 15, A.bitwise_and)
     ts(col("ci", 8), col("ci", 6), 1, A.bitwise_and)
-    ts(col("cf", 2), col("cf", 1), 15.0, A.is_lt, LIFT, A.mult)
-    ts(R("wa"), R("wj"), 0.0, A.is_equal, -DROP, A.mult)
     ts(col("ci", 10), col("ci", 8), 9.0, A.mult)
-    ts(R("wb"), R("wj"), 1.0, A.is_equal, LIFT, A.mult)
-    ts(col("cf", 3), col("cf", 2), 72.0, A.add)
     tt(col("ci", 11), col("ci", 10), col("ci", 9), A.add)
-    ts(R("ids"), R("idb"), col("cf", 0), A.add)
-    fill(R("cb", 128 + LOW, 5 * CB, CB), 0.0)
-    fill(col("cb", 5 * CB + 128 + width[5]), 0.0)
-    fill(col("cb", 6 * CB + 128 + width[6]), 0.0)
     ts(col("off16", 0), col("ci", 11), 0.5, A.mult, 7.0, A.min)
-    tt(R("wm"), R("wa"), R("wb"), A.add)
+    fill(col("cf", 3), 0.5)
     for b in range(4):
         ts(R("l4", 56 * b, 56 * b + 56), R("fvi"), 4.0, A.mult, float(b), A.add)
-    copy(R("l1"), R("fvi"))
     load("y", "wq", T.wc, [R("xs")], True)
-    load("y", "wsc", T.ws)
-    load("y", "wys", T.wy)
+    load("y", "wsc", T.ws, [R("xs")])
+    load("y", "wys", T.wy, [R("xs")])
 
-    def gather_h(t, q, b, c0, c1):
-        out = R("h%d" % t, 4 * c0 + b, 4 * c1, 4)
-        if t == 0:
-            scaled(q, out, (R("xs"), R("l4", 56 * b + c0 // 16, 56 * b + c1 // 16)), 1.0)
-        else:
-            scaled(q, out, (R("pl%d" % b, 0, V), R("l1", c0 // 16, c1 // 16)), 1.0 / 64)
+    parts = P["parts"]
+    spans, width = [], []
+    for j in range(TILES):
+        a, b = P["scalar"][j]
+        taken = sorted([(128 * j, 128 * j + 128), (a, b)])
+        runs = []
+        for lo, hi in parts:
+            at = lo
+            for c, d in taken:
+                if lo <= c < hi:
+                    if c > at:
+                        runs.append((at, c))
+                    at = d
+            if at < hi:
+                runs.append((at, hi))
+        spans.append(runs)
+        width.append(sum(d - c for c, d in runs))
+        ts(col("cb", CB * j + 128 + width[j]), col("ones", 0), float((b - a if b <= 128 * j else 0) - 2 * (F - 65)), A.mult)
+    fill(R("sb"), 0.0)
+    ts(R("ids"), R("idb"), col("cf", 0), A.add)
+
+    def gather_h(t, a, e):
+        for b in range(4):
+            out = R("h%d" % t, 4 * a + b, 4 * e, 4)
+            if t == 0:
+                scaled(out, (R("xs"), R("l4", 56 * b + a // 16, 56 * b + e // 16)))
+            else:
+                scaled(out, (R("pl%d" % b, 0, V), R("l1", a // 16, e // 16)), 1.0 / 64)
 
     def ranks(t):
-        h, qh, sh, ur, sr, neg = ("%s%d" % (n, t) for n in ("h", "qh", "sh", "ur", "sr", "neg"))
+        h, qh, sh, ur, sr, pos = ("%s%d" % (n, t) for n in ("h", "qh", "sh", "ur", "sr", "pos"))
         used = [128] * TILES
+        n = len(parts)
 
-        def row(bank, a, b):
-            mx(bank, b - a, R(ur), R(sr), R(qh, a, b), R(sh, a, b))
+        def seen(k, a, b, mine):
+            at = 512 * (k if mine else n + k) - parts[k][0]
+            return R("ps", at + a, at + b)
 
-        def column(bank, j):
-            mx(bank, 128, R(qh, 128 * j, 128 * j + 128), R(sh, 128 * j, 128 * j + 128), R(ur), R(sr))
+        def where(a):
+            return [k for k in range(n) if parts[k][0] <= a < parts[k][1]][0]
 
-        def v_count(j, a, b, shift=0):
-            edge = min(max(128 * j + 128, a), b)
-            for lo, hi, o in ((a, edge, A.is_ge), (edge, b, A.is_gt)):
-                if hi > lo:
-                    at = CB * j + used[j]
-                    ts(R("cb", at, at + hi - lo), R("ps", shift + lo, shift + hi), col(neg, j), A.add, 0.0, o)
-                    used[j] += hi - lo
+        def scores(k):
+            lo, hi = parts[k]
+            gather_h(t, lo, hi)
+            banks = P["pivots"][k]
+            quant(R(qh, lo, hi), R(sh, lo, hi), R(h, 4 * lo, 4 * hi))
+            for j, bank in zip(range(lo // 128, hi // 128), banks):
+                mx(bank, 128, R(qh, 128 * j, 128 * j + 128), R(sh, 128 * j, 128 * j + 128), R(ur), R(sr))
+            scaled(R(pos, lo // 128, hi // 128), R("ps", 512 * banks[0], 512 * banks[-1] + 1, 512))
+            for bank in (k, n + k):
+                mx(bank, hi - lo, R(ur), R(sr), R(qh, lo, hi), R(sh, lo, hi))
 
-        def v_equal(j, shift=0):
-            ts(R("eq", 128 * j, 128 * j + 128), R("ps", shift + 128 * j, shift + 128 * j + 128), col(neg, j), A.add, 0.0, A.is_equal)
+        def counts(k):
+            ready = lambda a, j: max(where(a), where(128 * j)) == k
+            for j in range(TILES):
+                own, s0, (a, b), into = 128 * j, SG * j, P["scalar"][j], col("sb", j)
+                if ready(own, j):
+                    act(R("sg", s0, s0 + 128), seen(k, own, own + 128, False), ACT.Sign, bias=col(pos, j), scale=-1.0, accum=col("sa", j))
+                    ts(R("eq", own, own + 128), R("sg", s0, s0 + 128), 0.0, A.is_equal)
+                    scan(R("cb", CB * j, CB * j + 128), R("hole"), R("eq", own, own + 128), 0.0, A.mult, A.subtract)
+                if ready(a, j):
+                    sg = R("sg", s0 + 128, s0 + 128 + b - a)
+                    act(sg, seen(where(a), a, b, False), ACT.Sign, bias=col(pos, j), scale=-1.0)
+                    if a > own:
+                        act(R("sg2", s0, s0 + b - a), sg, ACT.Relu, scale=-2.0, accum=into)
+                    else:
+                        act(R("sg2", s0, s0 + b - a), sg, ACT.Sign, bias=col("cf", 3), scale=-1.0, accum=into)
+                for c, d in spans[j]:
+                    if ready(c, j):
+                        at = CB * j + used[j]
+                        ts(R("cb", at, at + d - c), seen(where(c), c, d, True), col(pos, j), A.is_gt if c > own else A.is_ge, 2.0, A.mult)
+                        used[j] += d - c
 
-        def v_ties(j):
-            scan(R("cb", CB * j, CB * j + 128), R("hole"), R("eq", 128 * j, 128 * j + 128), 0.0, A.mult, A.subtract)
-
-        def v_sum(j, start):
-            at, w, end = CB * j + 127, width[j] // 2 + 1, SC * (SLOT[j] + 1)
-            scan(R("sc", end - w, end), R("cb", at, at + w), R("cb", at + w, at + 2 * w), float(start), A.add, A.add)
-
-        def s_sign(j, a, b):
-            act(R("sg", LOW * j, LOW * j + b - a), R("ps", a, b), ACT.Sign, bias=col(neg, j))
-
-        def s_count(j, a, b, sign, into, out=None):
-            r = R("sg", LOW * j + a, LOW * j + b)
-            act(out or r, r, ACT.Relu, scale=sign, accum=col(into, SLOT[j]))
-
-        high, mid = F - LOW, LOW // 2
-        quant(R(qh, LOW, F), R(sh, LOW, F), R(h, 4 * LOW, 4 * F))
-        for j in (4, 5, 6):
-            column(j - 2, j)
-        row(1, LOW, F)
-        gather_h(t, "s", 0, 0, LOW)
-        gather_h(t, "v", 3, 0, SPLIT[t])
-        gather_h(t, "s", 1, 0, LOW)
-        scaled("v", R(neg, 4, TILES), R("ps", 1024, 2560, 512), -1.0)
-        row(3, LOW, F)
-        gather_h(t, "v", 2, 0, mid)
-        gather_h(t, "s", 2, mid, LOW)
-        gather_h(t, "s", 3, SPLIT[t], LOW)
-        quant(R(qh, 0, mid), R(sh, 0, mid), R(h, 0, 4 * mid))
-        column(4, 0)
-        column(5, 1)
-        v_count(6, LOW, F, 1024)
-        quant(R(qh, mid, LOW), R(sh, mid, LOW), R(h, 4 * mid, 4 * LOW))
-        row(0, 0, LOW)
-        column(6, 2)
-        column(7, 3)
-        row(2, 0, LOW)
-        s_sign(4, LOW, F)
-        s_count(4, 128, high, 1.0, "al")
-        s_count(4, 0, 128, -1.0, "ae", R("sg", 4 * LOW + high, 5 * LOW))
-        scaled("s", R(neg, 0, 2), R("ps", 2048, 3072, 512), -1.0)
-        s_sign(1, LOW, F)
-        act(col("acc", 0), col("ae", 0), ACT.Identity, bias=col("al", 0), scale=-1.0)
-        s_count(1, 0, high, 1.0, "acc")
-        scaled("s", R(neg, 2, 4), R("ps", 3072, 4096, 512), -1.0)
-        s_sign(6, 1024, 1024 + LOW)
-        s_sign(5, 1024, 1024 + SHARE)
-        s_sign(2, LOW, F)
-        s_count(6, 0, LOW, -1.0, "ae")
-        s_count(5, 0, SHARE, -1.0, "ae")
-        s_sign(3, LOW, F)
-        act(R("acc", 1, 3), R("ae", 1, 3), ACT.Copy, scale=-1.0)
-        s_count(2, 0, high, 1.0, "acc")
-        s_count(3, 0, high, 1.0, "acc")
-        s_sign(0, LOW, F)
-        s_count(0, 0, high, 1.0, "acc")
-        v_equal(6, 1024)
-        v_equal(5, 1024)
-        v_count(5, LOW, F, 1024)
-        ts(R("eq", 512, 640), R("sg", 4 * LOW, 4 * LOW + 128), 0.0, A.is_equal)
-        v_ties(6)
-        v_ties(5)
-        v_count(4, 0, LOW)
-        v_ties(4)
-        v_sum(6, LOW)
-        v_count(5, SHARE, LOW)
-        for j in range(4):
-            v_equal(j)
-        v_sum(4, 128)
-        v_sum(5, SHARE)
-        for j in range(4):
-            v_ties(j)
-        v_count(1, 0, LOW)
-        v_count(2, 0, LOW)
-        v_sum(1, 0)
-        v_count(3, 0, LOW)
-        v_sum(2, 0)
-        v_count(0, 0, 128)
-        v_sum(3, 0)
-        v_count(0, 128, LOW)
-        tt(R("rk", 0, 6), R("sc", SC - 1, SC * 6, SC), R("acc", 0, 6), A.add)
-        v_sum(0, 0)
-        copy(R("ru", 0, 6), R("rk", 0, 6))
-        win = R("win%d" % t, 16, 16 + F)
-        copy((win, R("ru", 0, 6)), R("ids", 0, 96))
-        ts(col("ru", 6), col("sc", SC * TILES - 1), col("acc", 6), A.add)
-        copy((win, col("ru", 6)), R("ids", 96, K))
+        for k in range(n):
+            scores(k)
+            counts(k)
+        for j in range(TILES):
+            at, w, end = CB * j + 127, width[j] // 2 + 1, SC * (j + 1)
+            scan(R("sc", end - w, end), R("cb", at, at + w), R("cb", at + w, at + 2 * w), 0.0, A.add, A.add)
+        for a, b in P["runs"]:
+            tt(R("r1", a, b), R("sb", a, b), R("sa", a, b), A.subtract)
+            for j in range(a, b):
+                ts(col("ru", j), col("sc", SC * (j + 1) - 1), col("r1", j), A.add, -0.5, A.mult)
+            copy((R("win%d" % t), R("ru", a, b)), R("ids", 16 * a, 16 * b))
 
     def fired(t):
-        win, lst = "win%d" % t, "lst%d" % t
-        turn(R("tt", 0, 128), R(win, 16, 144))
-        turn(R("tt", 128, 256), R(win, 0, 128))
+        win, lst, at = "win%d" % t, "lst%d" % t, F - K
+        turn(R("tt", 0, 128), R(win, at, at + 128))
+        turn(R("tt", 128, 256), R(win, at - 16, at + 112))
         tt(R("q1"), R("tt", 0, 256, 32), R("tt", 16, 256, 32), A.add)
+        state["glue"] = lst
         tt(R("q2", p1=64), R("q1", p1=64), R("q1", p0=64), A.add)
         for a in range(4):
             tt(R("q3", p0=32 * a, p1=32 * a + 32), R("q2", p1=32), R("q2", p0=32, p1=64), A.add)
         copy(R(lst), (R("q3"), col("off16", 0)))
+        state["glue"] = None
         off = R(lst, 0, TILES)
         send(t, 0, R(lst, 0, 8), R("got%d" % t))
         pick_codes(R("slot%d" % t), R("qh%d" % t), off)
-        act(R("sls%d" % t), (R("sh%d" % t), off), ACT.Copy)
+        scaled(R("sls%d" % t), (R("sh%d" % t), off))
         send(t, 1, R("slot%d" % t), R("land%d" % t, 0, K), True)
         send(t, 2, R("sls%d" % t), R("lands%d" % t, 0, K))
 
     def report(t):
-        row = R("frow%d" % t)
-        copy(row, (R("cnt"), R("lst%d" % t, 0, TILES)))
+        rev, row = R("frev%d" % t), R("frow%d" % t)
+        scaled(rev, (R("cnt"), R("lst%d" % t, 0, TILES)))
+        scaled(row, (rev, R("rev", 0, TILES)))
         dma("y", lambda: T.fl[t:t + 1, :], lambda: ap(R(row[0], p1=1)), [row], [])
 
     def update(t):
-        got, g4, off = R("got%d" % t, 0, TILES), "g4%d" % t, R("ol%d" % t, 0, TILES)
-        tt(R("krow"), (R("fv256"), got), R("cnt", 0, K), A.add)
+        got, ow = R("got%d" % t, 0, TILES), R("ow%d" % t, 0, TILES)
+        tt(R("vm"), (R("fvt"), got), R("dm"), A.mult)
+        act(R("vrow"), (R("fvt"), got), ACT.Copy)
+        scan(R("own"), R("sm"), R("vm"), 0.0, A.mult, A.add)
+        ts(ow, R("own", 15, K, 16), -float(V), A.add)
+        for c in range(TILES):
+            mine = col("own", 16 * c + 15)
+            ts(R("ev", K * c + 16 * c, K * c + K), R("vrow", 16 * c, K), mine, A.is_equal, mine, A.mult)
+        scan(R("dd"), R("rm", 0, TILES * K), R("ev"), 0.0, A.mult, A.add)
+        ends = R("dd", K - 1, TILES * K, K)
         for b in range(4):
-            ts(R(g4, TILES * b, TILES * b + TILES), got, 4.0, A.mult, float(b), A.add)
-            if b == 1:
-                ts(R("kup"), R("krow"), col("cf", 3), A.add)
-                scan(R("ks"), R("wm"), R("krow"), 0.0, A.add, A.max)
-        at = [8 * c * (c + 1) for c in range(TILES + 1)]
-        ts(R("ab", 0, 16), R("kup", 0, 16), col("ks", 15), A.subtract)
-        tt(R("v256", 0, TILES), R("ks", 15, K, 16), R("kc", 0, TILES), A.subtract)
-        for c in range(TILES - 1, 0, -1):
-            act(R("ab", at[c], at[c + 1]), R("kup", 0, 16 * c + 16), ACT.Abs, bias=col("ks", 16 * c + 15), scale=-1.0)
-        for a in (0, 2):
-            act(R("x32", K * a, K * a + 2 * K), (R("h%d" % t), R(g4, TILES * a, TILES * a + 2 * TILES)), ACT.Copy, scale=32.0)
-        for c in (0, 6, 5, 4, 3, 2, 1):
-            src, out = R("ab", at[c], at[c + 1]), col("mm", c)
-            op("v", lambda src=src, out=out: g.vector.tensor_reduce(ap(out), ap(src), AxisListType.X, A.min, apply_absolute_value=True), [src], [out])
-        for b in range(4):
-            mx(2 + b, 128, R("wq", 128 * b, 128 * b + 128), R("wsc", 128 * b, 128 * b + 128), R("land%d" % t, 0, 128), R("lands%d" % t, 0, 128))
+            act(R("x32", K * b, K * b + K), (R("pl%d" % b, 0, V), ow), ACT.Copy, scale=0.5)
+            mx(4 + b, 128, R("wq", 128 * b, 128 * b + 128), R("wsc", 128 * b, 128 * b + 128), R("land%d" % t, 0, 128), R("lands%d" % t, 0, 128))
+            tt(R("n64", K * b, K * b + K), R("ps", 512 * (4 + b), 512 * (4 + b) + K), R("x32", K * b, K * b + K), A.add)
+        if t == 0:
+            off = R("ol0", 0, TILES)
+            ts(off, ends, -float(V), A.add)
+            for b in range(4):
+                copy((R("pl%d" % b), off), R("n64", K * b, K * b + K))
+        else:
+            for b in range(4):
+                scaled(R("nx", K * b, K * b + K), R("n64", K * b, K * b + K), 1.0 / 64)
+                ts(R("ol1", TILES * b, TILES * b + TILES), ends, 4.0, A.mult, float(b - 4 * V), A.add)
+            copy((R("xi"), R("ol1")), R("nx"))
 
-        def summed(b):
-            tt(R("n64", K * b, K * b + K), R("ps", 512 * (2 + b), 512 * (2 + b) + K), R("x32", K * b, K * b + K), A.add)
-        ts(R("t1", 0, TILES), R("mm", 0, TILES), 72.0, A.is_lt, 256.0 * V, A.mult)
-        summed(0)
-        tt(R("t2", 0, TILES), R("t1", 0, TILES), R("v256", 0, TILES), A.add)
-        summed(1)
-        ts(off, R("t2", 0, TILES), 1.0 / 256, A.mult)
-        summed(2)
-        for b in range(4):
-            copy((R("pl%d" % b), off), R("n64", K * b, K * b + K))
-            if b == 0:
-                summed(3)
-
-    gather_h(0, "s", 0, LOW, F)
-    gather_h(0, "v", 2, LOW, F)
-    gather_h(0, "s", 1, LOW, F)
     quant(R("qu"), R("su"), R("us"))
-    gather_h(0, "v", 3, LOW, F - 96)
-    gather_h(0, "s", 3, F - 96, F)
     pick_codes(R("ur0"), R("qu"), R("oz", 0, 8))
-    act(R("sr0"), (R("su"), R("oz", 0, 8)), ACT.Copy)
+    scaled(R("sr0"), (R("su"), R("oz", 0, 8)))
     ranks(0)
     fired(0)
-    scaled("s", R("fv256", 0, 640), (R("cnt", 0, V), R("l1", 0, 40)), 256.0)
-    scaled("v", R("fv256", 640, F), (R("cnt", 0, V), R("l1", 40, 56)), 256.0)
-    ts(R("kb", 0, TILES), R("cnt", 0, K, 16), col("cf", 1), A.add)
+    state["after"] = [R("lst0")]
+    copy(R("l1"), R("fvi"))
+    scaled(R("fvt", 0, 640), (R("cnt", V, F), R("l1", 0, 40)))
+    scaled(R("fvt", 640, F), (R("cnt", V, F), R("l1", 40, 56)))
     quant(R("land0", K, K + 128), R("lands0", K, K + 128), R("xs", 0, 512))
-    ts(R("kc", 0, TILES), R("kb", 0, TILES), col("cf", 2), A.add)
     for b in range(4):
-        scaled("vvvs"[b], R("pl%d" % b, 0, V), R("xs", b, 4 * V, 4), 64.0)
+        scaled(R("pl%d" % b, 0, V), R("xs", b, 4 * V, 4), 64.0)
     pick_codes(R("ur1"), R("qu"), R("oz", 8, 16))
-    act(R("sr1"), (R("su"), R("oz", 8, 16)), ACT.Copy)
+    scaled(R("sr1"), (R("su"), R("oz", 8, 16)))
+    state["after"] = []
+    iota(R("sm"), [[0, TILES], [1, 16]], 0, 0, False)
+    iota(R("win1", F - 128, F + 16), [[0, 144]], 0, 0, False)
+    iota(R("rvi"), [[-16, 8]], K - 1, 0)
+    ts(R("dm"), R("sm"), col("cf", 1), A.is_equal)
+    ts(R("sm"), R("sm"), 0.0, A.not_equal)
+    ts(R("rm", 0, 128), R("cnt", 0, 128), col("cf", 1), A.not_equal)
+    for a, b in ((128, 256), (256, 512), (512, F)):
+        copy(R("rm", a, b), R("rm", 0, b - a))
+    state["after"] = [R("lst0")]
+    ts(R("ev"), R("rm", 0, TILES * K), 0.0, A.mult)
+    state["after"] = []
+    ts(R("rev"), R("rvi"), col("cf", 1), A.subtract)
     update(0)
 
-    gather_h(1, "s", 0, LOW, F)
-    gather_h(1, "s", 1, LOW, F)
-    gather_h(1, "s", 2, LOW, F)
-    gather_h(1, "v", 3, LOW, F)
     ranks(1)
     fired(1)
+    state["after"] = [R("lst1")]
     quant(R("land1", K, K + 128), R("lands1", K, K + 128), R("xs", 0, 512))
+    for b in range(4):
+        scaled(R("xi", b, 4 * V, 4), R("pl%d" % b, 0, V), 1.0 / 64)
     report(0)
     report(1)
     quant(R("qwy"), R("swy"), R("wys"))
+    state["after"] = []
     update(1)
 
-    n = V // 2
-    for b in range(3):
-        scaled("s", R("xi", b, 4 * V, 4), R("pl%d" % b, 0, V), 1.0 / 64)
-    for a in (0, n):
-        scaled("v", R("xi", 4 * a + 3, 4 * (a + n), 4), R("pl3", a, a + n), 1.0 / 64)
-    for half in range(2):
-        a, b = n * half, n * half + n
-        q, s = R("qx", a, b), R("sx", a, b)
+    a = 0
+    for half, n in enumerate(P["out"]):
+        b = a + n
+        q, s, y = R("qx", a, b), R("sx", a, b), R("ysb", a, b)
         quant(q, s, R("xi", 4 * a, 4 * b))
         mx(half, n, R("qwy"), R("swy"), q, s)
         dma("y", lambda a=a, b=b: T.oc[:, 4 * a:4 * b], lambda q=q: ap(q).bitcast(dt.uint8), [q], [])
-
-    def store_scales(q, k):
+        scaled(y, R("ps", 512 * half, 512 * half + n))
+        dma("sy"[half % 2], lambda a=a, b=b: T.y[:, a:b], lambda y=y: ap(y), [y], [])
+        a = b
+    for k in range(4):
         s = R("sx", p0=32 * k, p1=32 * k + 4)
-        dma(q, lambda: T.osc[4 * k:4 * k + 4, :], lambda: ap(s), [s], [])
-
-    def store_y(q, half):
-        s = R("ysb", n * half, n * half + n)
-        dma(q, lambda: T.y[:, n * half:n * half + n], lambda: ap(s), [s], [])
-
-    act(R("ysb", 0, n), R("ps", 0, n), ACT.Copy)
-    copy(R("ysb", n, V), R("ps", 512, 512 + n))
-    store_y("s", 0)
-    store_scales("y", 0)
-    store_scales("y", 2)
-    store_y("y", 1)
-    store_scales("s", 1)
-    store_scales("s", 3)
-    _emit(g, T, ops)
+        dma("ys"[k % 2], lambda k=k: T.osc[4 * k:4 * k + 4, :], lambda s=s: ap(s), [s], [])
+    _emit(g, T, _order(ops))

@@ -2,16 +2,19 @@ from concourse.mybir import dt, AluOpType, ActivationFunctionType
 
 V, F, K, ROUNDS = 448, 896, 112, 2
 TILES = F // 128
-CB, SC, SG = 128 + F + 2, 450, 768
+CB, SC, SG = 784, 392, 768
 PL = 3 * V
 X4, U8, BF, F32, I32, U16, F16 = "float8_e4m3fn_x4", "uint8", "bfloat16", "float32", "int32", "uint16", "float16"
-P = {"parts": [(0, 384), (384, 640), (640, 896)],
-     "pivots": [[5, 6, 7], [6, 7], [6, 7]],
-     "scalar": [(384, 640), (640, 896), (640, 896), (640, 896), (640, 896), (0, 384), (0, 384)],
-     "runs": [(0, 4), (4, 7)],
-     "out": (224, 224)}
-QUEUES = "svvssvssvsvsssvvsssvvsssvsssvsssssvsvvssvvvsssssssssvv"
-ORDER = [0,1,5,37,22,2,3,36,4,30,34,9,11,14,12,163,33,13,31,35,32,6,15,8,24,26,17,25,16,164,23,38,18,27,42,45,10,28,7,29,39,44,43,67,40,19,46,41,69,68,48,165,47,66,49,20,93,51,90,52,70,50,92,168,21,71,60,72,61,75,91,65,74,56,57,73,94,62,76,58,83,80,99,53,96,77,88,98,103,95,81,63,79,105,59,101,54,97,64,82,104,100,106,78,85,115,84,107,55,125,109,124,102,126,86,114,116,108,110,130,123,112,87,89,133,134,117,119,131,121,111,113,132,127,118,128,122,120,135,136,129,137,138,139,140,141,142,143,169,144,145,148,153,170,147,154,166,171,158,172,155,167,157,161,149,151,146,174,175,156,160,176,159,181,183,178,184,177,180,179,189,182,150,186,185,152,192,190,187,195,193,191,198,162,196,188,194,200,197,201,228,204,199,202,205,203,206,254,227,207,230,251,213,229,253,209,210,208,252,212,231,211,255,233,218,232,214,226,236,223,234,235,217,237,260,215,222,241,257,221,246,224,256,219,264,244,259,266,240,258,262,216,242,247,270,239,265,225,220,243,238,261,277,282,263,285,249,267,280,286,271,248,284,273,245,291,275,268,278,287,274,293,272,279,276,292,269,295,294,250,281,283,289,296,288,297,290,299,298,300,301,302,303,304,173,305,306,309,308,322,316,315,310,314,312,307,327,326,323,328,318,325,333,332,334,335,329,336,330,341,331,317,311,338,337,313,347,339,344,342,348,340,345,343,350,349,351,352,346,356,357,353,355,354,319,358,320,321,324,359,364,360,361,365,370,366,362,371,367,363,368,372,369]
+R0 = {"gather": [(0, 384), (384, 640), (640, 896)], "quant": [(0, 384), (384, 640), (640, 896)],
+      "rows": [("v", 0, 384, 0), ("v", 384, 640, 1), ("v", 640, 896, 2), ("s", 0, 384, 3), ("s", 384, 640, 4), ("s", 640, 896, 5)],
+      "pivots": [(0, 3, 5), (3, 5, 6), (5, 7, 6)],
+      "scalar": [(384, 640), (640, 896), (640, 896), (640, 896), (640, 896), (0, 384), (0, 384)],
+      "ties": [(0, 3), (3, 5), (5, 7)], "runs": [(0, 4), (4, 7)]}
+R1 = dict(R0, scalar=[(384, 640), (384, 640), (640, 896), (0, 384), (640, 896), (0, 256), (0, 384)])
+P = {"rounds": [R0, R1], "out": (160, 160, 128),
+     "vm": [[(0, 4), (4, 7)]] * 2, "dd": [[(0, 3), (3, 7)]] * 2}
+QUEUES = "svsvsvsssvssvsssssssssssssssssvvvsssvssvssssssvssssssssssvvvv"
+ORDER = [3,5,0,1,37,2,38,11,13,4,15,193,195,39,22,9,150,12,24,25,36,23,192,14,18,29,19,42,41,26,27,197,34,28,198,43,47,196,6,44,30,52,32,149,31,46,53,8,48,45,56,58,51,49,57,66,69,54,59,50,7,80,75,61,72,60,199,70,77,86,35,83,67,55,33,62,73,81,87,88,71,93,82,63,74,40,64,108,68,84,92,96,94,78,109,89,110,91,65,79,111,103,116,76,98,95,102,106,99,101,85,114,118,90,107,112,104,97,120,113,100,122,119,115,117,121,105,126,124,123,128,125,127,139,16,129,141,17,131,130,20,140,132,21,133,153,134,135,136,154,145,155,158,151,10,137,156,138,194,148,147,152,144,157,142,159,160,165,164,162,161,166,168,167,163,170,171,172,169,176,175,173,174,177,143,178,179,185,146,183,181,180,186,187,184,182,188,189,200,190,191,201,204,202,203,205,206,212,207,209,210,216,217,213,215,208,225,218,228,211,245,219,220,229,234,231,242,214,236,221,239,232,240,227,268,237,226,255,252,230,247,235,222,233,223,246,248,256,269,253,270,224,250,238,241,251,243,274,257,266,264,262,260,244,271,267,263,276,258,275,278,272,249,282,277,280,273,254,261,265,281,279,286,283,284,259,288,304,287,285,301,299,289,305,302,291,290,306,300,292,293,303,294,296,295,310,297,298,314,311,316,312,307,317,315,319,313,320,318,326,328,327,325,323,324,321,322,330,329,333,331,335,337,334,332,336,338,341,344,339,346,340,343,342,345,308,347,309,348,358,353,350,349,359,360,366,354,351,365,361,364,355,356,352,363,362,357]
 
 
 def _scratch():
@@ -32,22 +35,22 @@ def _scratch():
     add(U8, 512, "wsc")
     add(F32, F, "cnt", "fvt")
     add(F32, K, "ids", "idb", "dm", "sm", "vrow", "vm", "own", "frev0", "frev1", "frow0", "frow1")
-    add(BF, 128, "ones", "hole")
+    add(BF, 512, "ones", "hole")
     add(I32, 16, "ci")
     add(I32, 8, "rvi")
-    add(F32, 8, "cf", "q1", "q2", "q3", "pos0", "pos1", "sa", "sb", "r1")
+    add(F32, 8, "cf", "q1", "q2", "q3", "pos0", "pos1", "sa", "sb")
     add(U16, 2, "off16")
-    add(U16, 8, "ru", "got0", "got1", "ol0", "ow0", "ow1", "rev")
-    add(U16, 28, "ol1")
+    add(U16, 8, "ru", "got0", "got1", "ol0", "rev")
+    add(U16, 28, "ol1", "ow0", "ow1")
     add(BF, 4 * F, "h0", "h1")
     add(X4, F, "qh0", "qh1")
     add(U8, F, "sh0", "sh1")
-    add(F16, TILES * CB, "cb")
+    add(BF, TILES * CB, "cb0", "cb1")
     add(F16, TILES * SC, "sc")
-    add(BF, F, "eq", "rm")
+    add(BF, F, "eq", "tie", "rm", "sgo")
     add(F16, TILES * K, "ev", "dd")
     add(BF, TILES * SG, "sg", "sg2")
-    add(F32, 16 + F, "win0", "win1")
+    add(F32, 2 * F + 32, "wa0", "wa1")
     add(F32, 256, "tt")
     add(X4, K, "slot0", "slot1")
     add(U8, K, "sls0", "sls1")
@@ -162,13 +165,10 @@ def _emit(g, T, ops):
             g.wait_ge(T.sem[name], total[name])
 
 
-def rank_program(g, core, T, topo):
-    rank = T.rank_of(core)
-    if rank is None:
-        return
+def _record(g, core, T, topo, rank):
     A, ACT = AluOpType, ActivationFunctionType
     ops = []
-    state = {"after": [], "glue": None, "copies": 0}
+    state = {"glue": None, "copies": 0}
 
     def R(name, c0=0, c1=None, step=1, p0=0, p1=128):
         if c1 is None:
@@ -184,7 +184,7 @@ def rank_program(g, core, T, topo):
         return T[r[0]][rows, r[3]:r[4]:r[5]] if r[5] > 1 else T[r[0]][rows, r[3]:r[4]]
 
     def op(q, f, reads, writes, kind="op", n=0):
-        rd, wr = list(state["after"]), []
+        rd, wr = [], []
         for r in reads:
             if isinstance(r, tuple):
                 rd += list(r) if len(r) == 2 else [r]
@@ -209,7 +209,7 @@ def rank_program(g, core, T, topo):
         op("v", lambda: g.vector.tensor_tensor(ap(out), ap(in0), ap(in1), o), [in0, in1], [out])
 
     def scan(out, d0, d1, init, op0, op1):
-        op("v", lambda: g.vector.tensor_tensor_scan(ap(out), ap(d0), ap(d1), init, op0, op1), [d0, d1], [out])
+        op("v", lambda: g.vector.tensor_tensor_scan(ap(out), ap(d0), ap(d1), ap(init), op0, op1), [d0, d1, init], [out])
 
     def fill(out, c):
         op("v", lambda: g.vector.memset(ap(out), c), [], [out])
@@ -226,12 +226,12 @@ def rank_program(g, core, T, topo):
         if accum is not None:
             kw["accum_out"] = accum
         op("s", lambda: g.scalar.activation(ap(out), ap(in_), func, **{k: ap(kw[k]) for k in kw}),
-           [in_, bias], [out] + ([accum] if accum is not None else []))
+           [in_, bias, scale], [out] + ([accum] if accum is not None else []))
 
     def scaled(out, in_, c=1.0):
         k = state["copies"]
         state["copies"] = k + 1
-        if QUEUES[k] == "s":
+        if QUEUES[k % len(QUEUES)] == "s":
             act(out, in_, ACT.Copy, scale=c)
         elif c == 1.0:
             copy(out, in_)
@@ -269,8 +269,10 @@ def rank_program(g, core, T, topo):
         n = len(topo.engines(core, peer))
         view = (lambda r: ap(r).bitcast(dt.uint8)) if codes else ap
         sem = "a%d" % (3 * t + k)
+        state["glue"] = sem
         op("g", lambda: g.remote_dma(view(dst), view(src), T.sem[sem], T.sem["sent"], pid, rid, topo.mask(core, peer)), [src], [], kind="remote", n=n)
-        ops.append({"q": "far", "r": [], "w": [dst], "sem": sem, "n": len(topo.engines(peer, core)), "kind": "far"})
+        ops.append({"q": "far", "r": [], "w": [dst], "sem": sem, "n": len(topo.engines(peer, core)), "kind": "far", "glue": sem})
+        state["glue"] = None
 
     def col(name, c):
         return R(name, c, c + 1)
@@ -281,49 +283,30 @@ def rank_program(g, core, T, topo):
     p = col("ci", 0)
     iota(p, [[0, 1]], 0, 1)
     iota(R("idb"), [[128, TILES], [1, 16]], 0, 0, False)
-    iota(R("ones"), [[0, 128]], 1, 0, False)
-    op("g", lambda: g.affine_select(ap(R("hole")), ap(R("ones")), [[-1, 128]], A.not_equal, -1.0, 0, 1), [R("ones")], [R("hole")])
+    wide = 128 * max(b - a for c in P["rounds"] for a, b in c["ties"])
+    fill(R("ones", 0, wide), 1.0)
+    op("g", lambda: g.affine_select(ap(R("hole", 0, wide)), ap(R("ones", 0, wide)), [[0, wide // 128], [-1, 128]], A.not_equal, -1.0, 0, 1),
+       [R("ones", 0, wide)], [R("hole", 0, wide)])
+    fill(R("hole", 0, wide, 128), 0.0)
     iota(R("cnt"), [[1, F]], 0, 0, False)
     fill(R("oz", 0, 8), 0)
     fill(R("oz", 8, 16), 1)
-    iota(R("win0", F - 128, F + 16), [[0, 144]], 0, 0, False)
-    ts(col("ci", 1), p, 7, A.bitwise_and)
     ts(col("ci", 3), p, 4, A.arith_shift_right, 1, A.bitwise_and)
     ts(col("ci", 4), p, 112, A.bitwise_and)
     ts(col("ci", 5), p, 15, A.bitwise_and)
     copy(R("cf", 0, 2), R("ci", 4, 6))
-    tt(col("ci", 6), col("ci", 1), col("ci", 3), A.add)
-    tt(col("ci", 9), col("ci", 1), col("ci", 3), A.subtract)
-    ts(col("ci", 8), col("ci", 6), 1, A.bitwise_and)
-    ts(col("ci", 10), col("ci", 8), 9.0, A.mult)
-    tt(col("ci", 11), col("ci", 10), col("ci", 9), A.add)
-    ts(col("off16", 0), col("ci", 11), 0.5, A.mult, 7.0, A.min)
-    fill(col("cf", 3), 0.5)
+    tt(col("ci", 6), col("ci", 5), col("ci", 3), A.subtract)
+    ts(col("ci", 7), col("ci", 6), 1.0, A.add)
+    ts(col("ci", 8), col("ci", 7), 1, A.arith_shift_right)
+    ts(col("ci", 9), col("ci", 6), 1, A.bitwise_and)
+    ts(col("ci", 10), col("ci", 9), 4.0, A.mult)
+    tt(col("ci", 12), col("ci", 10), col("ci", 8), A.add)
+    ts(col("off16", 0), col("ci", 12), 7.0, A.min)
     for b in range(4):
         ts(R("l4", 56 * b, 56 * b + 56), R("fvi"), 4.0, A.mult, float(b), A.add)
     load("y", "wq", T.wc, [R("xs")], True)
     load("y", "wsc", T.ws, [R("xs")])
     load("y", "wys", T.wy, [R("xs")])
-
-    parts = P["parts"]
-    spans, width = [], []
-    for j in range(TILES):
-        a, b = P["scalar"][j]
-        taken = sorted([(128 * j, 128 * j + 128), (a, b)])
-        runs = []
-        for lo, hi in parts:
-            at = lo
-            for c, d in taken:
-                if lo <= c < hi:
-                    if c > at:
-                        runs.append((at, c))
-                    at = d
-            if at < hi:
-                runs.append((at, hi))
-        spans.append(runs)
-        width.append(sum(d - c for c, d in runs))
-        ts(col("cb", CB * j + 128 + width[j]), col("ones", 0), float((b - a if b <= 128 * j else 0) - 2 * (F - 65)), A.mult)
-    fill(R("sb"), 0.0)
     ts(R("ids"), R("idb"), col("cf", 0), A.add)
 
     def gather_h(t, a, e):
@@ -335,65 +318,65 @@ def rank_program(g, core, T, topo):
                 scaled(out, (R("pl%d" % b, 0, V), R("l1", a // 16, e // 16)), 1.0 / 64)
 
     def ranks(t):
-        h, qh, sh, ur, sr, pos = ("%s%d" % (n, t) for n in ("h", "qh", "sh", "ur", "sr", "pos"))
-        used = [128] * TILES
-        n = len(parts)
+        c = P["rounds"][t]
+        h, qh, sh, ur, sr, pos, cb, win = ("%s%d" % (n, t) for n in ("h", "qh", "sh", "ur", "sr", "pos", "cb", "wa"))
+        iota(R(win, 2 * (F - 128), 2 * (F + 16)), [[0, 288]], 0, 0, False)
 
-        def seen(k, a, b, mine):
-            at = 512 * (k if mine else n + k) - parts[k][0]
-            return R("ps", at + a, at + b)
+        def seen(e, a, b):
+            lo, bank = [(r[1], r[3]) for r in c["rows"] if r[0] == e and r[1] <= a and b <= r[2]][0]
+            return R("ps", 512 * bank + a - lo, 512 * bank + b - lo)
 
-        def where(a):
-            return [k for k in range(n) if parts[k][0] <= a < parts[k][1]][0]
-
-        def scores(k):
-            lo, hi = parts[k]
-            gather_h(t, lo, hi)
-            banks = P["pivots"][k]
-            quant(R(qh, lo, hi), R(sh, lo, hi), R(h, 4 * lo, 4 * hi))
-            for j, bank in zip(range(lo // 128, hi // 128), banks):
-                mx(bank, 128, R(qh, 128 * j, 128 * j + 128), R(sh, 128 * j, 128 * j + 128), R(ur), R(sr))
-            scaled(R(pos, lo // 128, hi // 128), R("ps", 512 * banks[0], 512 * banks[-1] + 1, 512))
-            for bank in (k, n + k):
-                mx(bank, hi - lo, R(ur), R(sr), R(qh, lo, hi), R(sh, lo, hi))
-
-        def counts(k):
-            ready = lambda a, j: max(where(a), where(128 * j)) == k
-            for j in range(TILES):
-                own, s0, (a, b), into = 128 * j, SG * j, P["scalar"][j], col("sb", j)
-                if ready(own, j):
-                    act(R("sg", s0, s0 + 128), seen(k, own, own + 128, False), ACT.Sign, bias=col(pos, j), scale=-1.0, accum=col("sa", j))
-                    ts(R("eq", own, own + 128), R("sg", s0, s0 + 128), 0.0, A.is_equal)
-                    scan(R("cb", CB * j, CB * j + 128), R("hole"), R("eq", own, own + 128), 0.0, A.mult, A.subtract)
-                if ready(a, j):
-                    sg = R("sg", s0 + 128, s0 + 128 + b - a)
-                    act(sg, seen(where(a), a, b, False), ACT.Sign, bias=col(pos, j), scale=-1.0)
-                    if a > own:
-                        act(R("sg2", s0, s0 + b - a), sg, ACT.Relu, scale=-2.0, accum=into)
-                    else:
-                        act(R("sg2", s0, s0 + b - a), sg, ACT.Sign, bias=col("cf", 3), scale=-1.0, accum=into)
-                for c, d in spans[j]:
-                    if ready(c, j):
-                        at = CB * j + used[j]
-                        ts(R("cb", at, at + d - c), seen(where(c), c, d, True), col(pos, j), A.is_gt if c > own else A.is_ge, 2.0, A.mult)
-                        used[j] += d - c
-
-        for k in range(n):
-            scores(k)
-            counts(k)
+        spans, width = [], []
         for j in range(TILES):
-            at, w, end = CB * j + 127, width[j] // 2 + 1, SC * (j + 1)
-            scan(R("sc", end - w, end), R("cb", at, at + w), R("cb", at + w, at + 2 * w), 0.0, A.add, A.add)
-        for a, b in P["runs"]:
-            tt(R("r1", a, b), R("sb", a, b), R("sa", a, b), A.subtract)
+            taken = sorted([c["scalar"][j], (128 * j, 128 * j + 128)])
+            runs = []
+            for e, a, b, bank in c["rows"]:
+                if e == "v":
+                    for x, y in taken:
+                        if x < b and y > a:
+                            if x > a:
+                                runs.append((a, x))
+                            a = max(a, y)
+                    if a < b:
+                        runs.append((a, b))
+            spans.append(runs)
+            width.append(sum(b - a for a, b in runs))
+            a, b = c["scalar"][j]
+            k = 2 * (F - 65 - (b - a if a < 128 * j else 0))
+            iota(R(cb, CB * j + width[j], CB * j + width[j] + 2), [[k % 16 - k // 16 * 16, 2]], k // 16 * 16, 0, False)
+        for a, b in c["gather"]:
+            gather_h(t, a, b)
+        for a, b in c["quant"]:
+            quant(R(qh, a, b), R(sh, a, b), R(h, 4 * a, 4 * b))
+        for a, b, bank in c["pivots"]:
             for j in range(a, b):
-                ts(col("ru", j), col("sc", SC * (j + 1) - 1), col("r1", j), A.add, -0.5, A.mult)
-            copy((R("win%d" % t), R("ru", a, b)), R("ids", 16 * a, 16 * b))
+                mx(bank + j - a, 128, R(qh, 128 * j, 128 * j + 128), R(sh, 128 * j, 128 * j + 128), R(ur), R(sr))
+            scaled(R(pos, a, b), R("ps", 512 * bank, 512 * (bank + b - a - 1) + 1, 512))
+        for e, a, b, bank in c["rows"]:
+            mx(bank, b - a, R(ur), R(sr), R(qh, a, b), R(sh, a, b))
+        for j in range(TILES):
+            own, pv, (a, b) = 128 * j, col(pos, j), c["scalar"][j]
+            act(R("sgo", own, own + 128), seen("s", own, own + 128), ACT.Sign, bias=pv, scale=-1.0, accum=col("sa", j))
+            act(R("sg", SG * j, SG * j + b - a), seen("s", a, b), ACT.Sign, bias=pv, scale=-1.0)
+            act(R("sg2", SG * j, SG * j + b - a), R("sg", SG * j, SG * j + b - a), ACT.Relu, scale=2.0 if a < own else -2.0, accum=col("sb", j))
+            at = CB * j
+            for a, b in spans[j]:
+                ts(R(cb, at, at + b - a), seen("v", a, b), pv, A.is_ge if a < own else A.is_gt, -2.0, A.mult)
+                at += b - a
+        for a, b in c["ties"]:
+            ts(R("eq", 128 * a, 128 * b), R("sgo", 128 * a, 128 * b), 0.0, A.is_equal)
+            scan(R("tie", 128 * a, 128 * b), R("hole", 0, 128 * (b - a)), R("eq", 128 * a, 128 * b), 0.0, A.mult, A.add)
+        for j in range(TILES):
+            at, w, end = CB * j, width[j] // 2 + 1, SC * (j + 1)
+            scan(R("sc", end - w, end), R(cb, at, at + w), R(cb, at + w, at + 2 * w), col("tie", 128 * j + 127), A.add, A.add)
+            ts(col("ru", j), col("sc", end - 1), col("sa", j), A.add, col("sb", j), A.add if c["scalar"][j][0] < 128 * j else A.subtract)
+        for a, b in c["runs"]:
+            copy((R(win), R("ru", a, b)), R("ids", 16 * a, 16 * b))
 
     def fired(t):
-        win, lst, at = "win%d" % t, "lst%d" % t, F - K
-        turn(R("tt", 0, 128), R(win, at, at + 128))
-        turn(R("tt", 128, 256), R(win, at - 16, at + 112))
+        win, lst, at = "wa%d" % t, "lst%d" % t, 2 * (F - K)
+        turn(R("tt", 0, 128), R(win, at, at + 256, 2))
+        turn(R("tt", 128, 256), R(win, at - 32, at + 224, 2))
         tt(R("q1"), R("tt", 0, 256, 32), R("tt", 16, 256, 32), A.add)
         state["glue"] = lst
         tt(R("q2", p1=64), R("q1", p1=64), R("q1", p0=64), A.add)
@@ -415,18 +398,22 @@ def rank_program(g, core, T, topo):
         dma("y", lambda: T.fl[t:t + 1, :], lambda: ap(R(row[0], p1=1)), [row], [])
 
     def update(t):
-        got, ow = R("got%d" % t, 0, TILES), R("ow%d" % t, 0, TILES)
-        tt(R("vm"), (R("fvt"), got), R("dm"), A.mult)
-        act(R("vrow"), (R("fvt"), got), ACT.Copy)
-        scan(R("own"), R("sm"), R("vm"), 0.0, A.mult, A.add)
-        ts(ow, R("own", 15, K, 16), -float(V), A.add)
+        got, ow = R("got%d" % t, 0, TILES), "ow%d" % t
+        scaled(R("vrow"), (R("fvt"), got))
+        for a, b in P["vm"][t]:
+            tt(R("vm", 16 * a, 16 * b), (R("fvt"), R(got[0], a, b)), R("dm", 16 * a, 16 * b), A.mult)
+            scan(R("own", 16 * a, 16 * b), R("sm", 16 * a, 16 * b), R("vm", 16 * a, 16 * b), 0.0, A.mult, A.add)
+        for b in range(4):
+            ts(R(ow, TILES * b, TILES * b + TILES), got, 4.0, A.mult, float(b), A.add)
+        for a, b in ((0, 2), (2, 4)):
+            scaled(R("x32", K * a, K * b), (R("h%d" % t), R(ow, TILES * a, TILES * b)), 32.0)
         for c in range(TILES):
             mine = col("own", 16 * c + 15)
             ts(R("ev", K * c + 16 * c, K * c + K), R("vrow", 16 * c, K), mine, A.is_equal, mine, A.mult)
-        scan(R("dd"), R("rm", 0, TILES * K), R("ev"), 0.0, A.mult, A.add)
+        for a, b in P["dd"][t]:
+            scan(R("dd", 128 * a, K * b), R("rm", 128 * a, K * b), R("ev", 128 * a, K * b), 0.0, A.mult, A.add)
         ends = R("dd", K - 1, TILES * K, K)
         for b in range(4):
-            act(R("x32", K * b, K * b + K), (R("pl%d" % b, 0, V), ow), ACT.Copy, scale=0.5)
             mx(4 + b, 128, R("wq", 128 * b, 128 * b + 128), R("wsc", 128 * b, 128 * b + 128), R("land%d" % t, 0, 128), R("lands%d" % t, 0, 128))
             tt(R("n64", K * b, K * b + K), R("ps", 512 * (4 + b), 512 * (4 + b) + K), R("x32", K * b, K * b + K), A.add)
         if t == 0:
@@ -445,40 +432,33 @@ def rank_program(g, core, T, topo):
     scaled(R("sr0"), (R("su"), R("oz", 0, 8)))
     ranks(0)
     fired(0)
-    state["after"] = [R("lst0")]
     copy(R("l1"), R("fvi"))
-    scaled(R("fvt", 0, 640), (R("cnt", V, F), R("l1", 0, 40)))
-    scaled(R("fvt", 640, F), (R("cnt", V, F), R("l1", 40, 56)))
+    scaled(R("fvt", 0, V), (R("cnt", V, F), R("l1", 0, 28)))
+    scaled(R("fvt", V, F), (R("cnt", V, F), R("l1", 28, 56)))
     quant(R("land0", K, K + 128), R("lands0", K, K + 128), R("xs", 0, 512))
     for b in range(4):
         scaled(R("pl%d" % b, 0, V), R("xs", b, 4 * V, 4), 64.0)
     pick_codes(R("ur1"), R("qu"), R("oz", 8, 16))
     scaled(R("sr1"), (R("su"), R("oz", 8, 16)))
-    state["after"] = []
     iota(R("sm"), [[0, TILES], [1, 16]], 0, 0, False)
-    iota(R("win1", F - 128, F + 16), [[0, 144]], 0, 0, False)
     iota(R("rvi"), [[-16, 8]], K - 1, 0)
     ts(R("dm"), R("sm"), col("cf", 1), A.is_equal)
     ts(R("sm"), R("sm"), 0.0, A.not_equal)
     ts(R("rm", 0, 128), R("cnt", 0, 128), col("cf", 1), A.not_equal)
     for a, b in ((128, 256), (256, 512), (512, F)):
         copy(R("rm", a, b), R("rm", 0, b - a))
-    state["after"] = [R("lst0")]
     ts(R("ev"), R("rm", 0, TILES * K), 0.0, A.mult)
-    state["after"] = []
     ts(R("rev"), R("rvi"), col("cf", 1), A.subtract)
     update(0)
 
     ranks(1)
     fired(1)
-    state["after"] = [R("lst1")]
     quant(R("land1", K, K + 128), R("lands1", K, K + 128), R("xs", 0, 512))
     for b in range(4):
         scaled(R("xi", b, 4 * V, 4), R("pl%d" % b, 0, V), 1.0 / 64)
     report(0)
     report(1)
     quant(R("qwy"), R("swy"), R("wys"))
-    state["after"] = []
     update(1)
 
     a = 0
@@ -494,4 +474,10 @@ def rank_program(g, core, T, topo):
     for k in range(4):
         s = R("sx", p0=32 * k, p1=32 * k + 4)
         dma("ys"[k % 2], lambda k=k: T.osc[4 * k:4 * k + 4, :], lambda s=s: ap(s), [s], [])
-    _emit(g, T, _order(ops))
+    return ops
+
+
+def rank_program(g, core, T, topo):
+    rank = T.rank_of(core)
+    if rank is not None:
+        _emit(g, T, _order(_record(g, core, T, topo, rank)))

from concourse.mybir import dt, AluOpType, ActivationFunctionType

V, F, K, ROUNDS = 448, 896, 112, 2
TILES = F // 128
CB, SC, SG = 784, 392, 768
PL = 3 * V
X4, U8, BF, F32, I32, U16, F16 = "float8_e4m3fn_x4", "uint8", "bfloat16", "float32", "int32", "uint16", "float16"
R0 = {"gather": [(0, 384), (384, 640), (640, 896)], "quant": [(0, 384), (384, 640), (640, 896)],
      "rows": [("v", 0, 384, 0), ("v", 384, 640, 1), ("v", 640, 896, 2), ("s", 0, 384, 3), ("s", 384, 640, 4), ("s", 640, 896, 5)],
      "pivots": [(0, 3, 5), (3, 5, 6), (5, 7, 6)],
      "scalar": [(384, 640), (640, 896), (640, 896), (640, 896), (640, 896), (0, 384), (0, 384)],
      "ties": [(0, 3), (3, 5), (5, 7)], "runs": [(0, 4), (4, 7)]}
R1 = dict(R0, scalar=[(384, 640), (384, 640), (640, 896), (0, 384), (640, 896), (0, 256), (0, 384)])
P = {"rounds": [R0, R1], "out": (160, 160, 128),
     "vm": [[(0, 4), (4, 7)]] * 2, "dd": [[(0, 3), (3, 7)]] * 2}
QUEUES = "svsvsvsssvssvsssssssssssssssssvvvsssvssvssssssvssssssssssvvvv"
ORDER = [3,5,0,1,37,2,38,11,13,4,15,193,195,39,22,9,150,12,24,25,36,23,192,14,18,29,19,42,41,26,27,197,34,28,198,43,47,196,6,44,30,52,32,149,31,46,53,8,48,45,56,58,51,49,57,66,69,54,59,50,7,80,75,61,72,60,199,70,77,86,35,83,67,55,33,62,73,81,87,88,71,93,82,63,74,40,64,108,68,84,92,96,94,78,109,89,110,91,65,79,111,103,116,76,98,95,102,106,99,101,85,114,118,90,107,112,104,97,120,113,100,122,119,115,117,121,105,126,124,123,128,125,127,139,16,129,141,17,131,130,20,140,132,21,133,153,134,135,136,154,145,155,158,151,10,137,156,138,194,148,147,152,144,157,142,159,160,165,164,162,161,166,168,167,163,170,171,172,169,176,175,173,174,177,143,178,179,185,146,183,181,180,186,187,184,182,188,189,200,190,191,201,204,202,203,205,206,212,207,209,210,216,217,213,215,208,225,218,228,211,245,219,220,229,234,231,242,214,236,221,239,232,240,227,268,237,226,255,252,230,247,235,222,233,223,246,248,256,269,253,270,224,250,238,241,251,243,274,257,266,264,262,260,244,271,267,263,276,258,275,278,272,249,282,277,280,273,254,261,265,281,279,286,283,284,259,288,304,287,285,301,299,289,305,302,291,290,306,300,292,293,303,294,296,295,310,297,298,314,311,316,312,307,317,315,319,313,320,318,326,328,327,325,323,324,321,322,330,329,333,331,335,337,334,332,336,338,341,344,339,346,340,343,342,345,308,347,309,348,358,353,350,349,359,360,366,354,351,365,361,364,355,356,352,363,362,357]


def _scratch():
    s = {}
    def add(dtype, cols, *names):
        for n in names:
            s[n] = ("sbuf", [128, cols], dtype)
    add(BF, 4 * V, "xs")
    add(BF, 4 * PL, "xi")
    add(I32, 56, "fvi")
    add(BF, 512, "us", "wys")
    add(U16, 224, "l4")
    add(U16, 56, "l1")
    add(X4, 128, "qu", "qwy", "ur0", "ur1")
    add(U8, 128, "su", "swy", "sr0", "sr1")
    add(U16, 16, "oz", "lst0", "lst1")
    add(X4, 512, "wq")
    add(U8, 512, "wsc")
    add(F32, F, "cnt", "fvt")
    add(F32, K, "ids", "idb", "dm", "sm", "vrow", "vm", "own", "frev0", "frev1", "frow0", "frow1")
    add(BF, 512, "ones", "hole")
    add(I32, 16, "ci")
    add(I32, 8, "rvi")
    add(F32, 8, "cf", "q1", "q2", "q3", "pos0", "pos1", "sa", "sb")
    add(U16, 2, "off16")
    add(U16, 8, "ru", "got0", "got1", "ol0", "rev")
    add(U16, 28, "ol1", "ow0", "ow1")
    add(BF, 4 * F, "h0", "h1")
    add(X4, F, "qh0", "qh1")
    add(U8, F, "sh0", "sh1")
    add(BF, TILES * CB, "cb0", "cb1")
    add(F16, TILES * SC, "sc")
    add(BF, F, "eq", "tie", "rm", "sgo")
    add(F16, TILES * K, "ev", "dd")
    add(BF, TILES * SG, "sg", "sg2")
    add(F32, 2 * F + 32, "wa0", "wa1")
    add(F32, 256, "tt")
    add(X4, K, "slot0", "slot1")
    add(U8, K, "sls0", "sls1")
    add(X4, K + 128, "land0", "land1")
    add(U8, K + 128, "lands0", "lands1")
    add(F32, 4 * K, "x32")
    add(BF, 4 * K, "n64", "nx")
    add(BF, PL, "pl0", "pl1", "pl2", "pl3")
    add(X4, V, "qx")
    add(U8, V, "sx")
    add(F32, V, "ysb")
    s["ps"] = ("psum", [128, 4096], F32)
    return s


SCRATCH = _scratch()
POOL = {"v": 56, "s": 40, "t": 14, "g": 12}
DMAS = 20
SEMAPHORES = ([q + str(i) for q in POOL for i in range(POOL[q])] + ["d%d" % i for i in range(DMAS)]
              + ["a%d" % i for i in range(3 * ROUNDS)] + ["sent"])


def _meet(a, b):
    if a[0] != b[0]:
        return False
    if a[0] == "ps":
        return a[3] // 512 <= (b[4] - 1) // 512 and b[3] // 512 <= (a[4] - 1) // 512
    if a[1] >= b[2] or b[1] >= a[2] or a[3] >= b[4] or b[3] >= a[4]:
        return False
    if a[5] == b[5]:
        return (a[3] - b[3]) % a[5] == 0
    if a[5] == 1:
        a, b = b, a
    if b[5] == 1:
        return (a[3] - b[3]) % a[5] < b[4] - b[3]
    return True


def _hazard(o, e):
    return any(_meet(a, b) for a in o["r"] + o["w"] for b in e["w"]) or any(_meet(a, b) for a in o["w"] for b in e["r"])


def _units(ops):
    units = []
    for o in ops:
        if o.get("glue") and units and units[-1][-1].get("glue") == o["glue"]:
            units[-1].append(o)
        else:
            units.append([o])
    return units


def _order(ops):
    units = _units(ops)
    assert sorted(ORDER) == list(range(len(units)))
    return [o for i in ORDER for o in units[i]]


def _emit(g, T, ops):
    queue = {"v": g.vector, "s": g.scalar, "t": g.tensor, "g": g, "y": g.sync}
    known = {q: 0 for q in queue}
    seen, waits, needed = [], [], set()
    for i, o in enumerate(ops):
        q, deps = o["q"], []
        if q != "far":
            for j in range(i - 1, -1, -1):
                if known[q] >> j & 1:
                    continue
                e = ops[j]
                hit = _hazard(o, e)
                if not hit and e["q"] != q:
                    hit = any(a[0] == "ps" and _meet(a, b) for a in o["r"] for b in e["r"])
                if hit:
                    deps.append(j)
                    needed.add(j)
                    known[q] |= seen[j] | 1 << j
        waits.append(deps)
        seen.append(known[q] if q != "far" else 0)
    last = {q: [[-1, 0] for k in range(POOL[q])] for q in POOL}
    mark, total, dmas = {}, {}, [0]
    for i, o in enumerate(ops):
        q = o["q"]
        if q == "far":
            mark[i] = (o["sem"], o["n"])
            total[o["sem"]] = o["n"]
            continue
        for j in reversed(waits[i]):
            queue[q].wait_ge(T.sem[mark[j][0]], mark[j][1])
        call = o["f"]()
        if o["kind"] == "dma":
            name = "d%d" % dmas[0]
            dmas[0] += 1
            call.then_inc(T.sem[name], 16)
            mark[i] = (name, 16)
            total[name] = 16
        elif o["kind"] == "remote":
            total["sent"] = total.get("sent", 0) + o["n"]
        elif i in needed:
            free = [k for k in range(POOL[q]) if last[q][k][0] < 0 or seen[i] >> last[q][k][0] & 1]
            k = min(free or range(POOL[q]), key=lambda z: last[q][z][0])
            last[q][k] = [i, last[q][k][1] + 1]
            name = q + str(k)
            call.then_inc(T.sem[name], 1)
            mark[i] = (name, last[q][k][1])
            total[name] = last[q][k][1]
    waited = {}
    for i, o in enumerate(ops):
        for j in waits[i]:
            waited[mark[j][0]] = max(waited.get(mark[j][0], 0), mark[j][1])
    for name in sorted(total, key=lambda z: z[0] == "d"):
        if waited.get(name, 0) < total[name]:
            g.wait_ge(T.sem[name], total[name])


def _record(g, core, T, topo, rank):
    A, ACT = AluOpType, ActivationFunctionType
    ops = []
    state = {"glue": None, "copies": 0}

    def R(name, c0=0, c1=None, step=1, p0=0, p1=128):
        if c1 is None:
            c1 = SCRATCH[name][1][1]
        return (name, p0, p1, c0, c1 - (c1 - c0 - 1) % step, step)

    def ap(r):
        if not isinstance(r, tuple):
            return r
        if len(r) == 2:
            return ap(r[0]).indirect(ap(r[1]))
        rows = slice(None) if (r[1], r[2]) == (0, 128) else slice(r[1], r[2])
        return T[r[0]][rows, r[3]:r[4]:r[5]] if r[5] > 1 else T[r[0]][rows, r[3]:r[4]]

    def op(q, f, reads, writes, kind="op", n=0):
        rd, wr = [], []
        for r in reads:
            if isinstance(r, tuple):
                rd += list(r) if len(r) == 2 else [r]
        for w in writes:
            if len(w) == 2:
                wr.append(w[0])
                rd.append(w[1])
            else:
                wr.append(w)
        ops.append({"q": q, "f": f, "r": rd, "w": wr, "kind": kind, "n": n, "glue": state["glue"]})

    def copy(out, in_):
        op("v", lambda: g.vector.tensor_copy(ap(out), ap(in_)), [in_], [out])

    def ts(out, in0, s1, op0, s2=None, op1=None):
        if op1 is None:
            op("v", lambda: g.vector.tensor_scalar(ap(out), ap(in0), ap(s1), None, op0), [in0, s1], [out])
        else:
            op("v", lambda: g.vector.tensor_scalar(ap(out), ap(in0), ap(s1), ap(s2), op0, op1), [in0, s1, s2], [out])

    def tt(out, in0, in1, o):
        op("v", lambda: g.vector.tensor_tensor(ap(out), ap(in0), ap(in1), o), [in0, in1], [out])

    def scan(out, d0, d1, init, op0, op1):
        op("v", lambda: g.vector.tensor_tensor_scan(ap(out), ap(d0), ap(d1), ap(init), op0, op1), [d0, d1, init], [out])

    def fill(out, c):
        op("v", lambda: g.vector.memset(ap(out), c), [], [out])

    def turn(out, in_):
        op("v", lambda: g.vector.transpose(ap(out), ap(in_)), [in_], [out])

    def act(out, in_, func, bias=0.0, scale=1.0, accum=None):
        kw = {}
        if isinstance(bias, tuple):
            kw["bias"] = bias
        if scale != 1.0:
            kw["scale"] = scale
        if accum is not None:
            kw["accum_out"] = accum
        op("s", lambda: g.scalar.activation(ap(out), ap(in_), func, **{k: ap(kw[k]) for k in kw}),
           [in_, bias, scale], [out] + ([accum] if accum is not None else []))

    def scaled(out, in_, c=1.0):
        k = state["copies"]
        state["copies"] = k + 1
        if QUEUES[k % len(QUEUES)] == "s":
            act(out, in_, ACT.Copy, scale=c)
        elif c == 1.0:
            copy(out, in_)
        else:
            ts(out, in_, c, A.mult)
        ops[-1]["either"] = k

    def quant(q, s, in_):
        op("v", lambda: g.vector.quantize_mx(ap(q), ap(s), ap(in_)), [in_], [q, s])

    def mx(bank, n, lq, ls, rq, rs):
        out = R("ps", 512 * bank, 512 * bank + n)
        op("t", lambda: g.tensor.matmul_mx(ap(out), ap(lq), ap(ls), ap(rq), ap(rs), True, True), [lq, ls, rq, rs], [out])

    def pick_codes(out, win, off):
        op("v", lambda: g.vector.tensor_copy(ap(out).bitcast(dt.uint32), ap(win).bitcast(dt.uint32).indirect(ap(off))), [win, off], [out])

    def iota(out, pattern, base, mult, exact=True):
        if exact:
            op("g", lambda: g.iota(ap(out), pattern, base, mult), [], [out])
        else:
            op("g", lambda: g.iota(ap(out), pattern, base, mult, allow_small_or_imprecise_dtypes=True), [], [out])

    def dma(q, out, in_, reads, writes):
        e = g.sync if q == "y" else g.scalar
        op(q, lambda: e.dma_start(out(), in_()), reads, writes, kind="dma")

    def load(q, name, src, after=(), codes=False):
        r = R(name)
        dma(q, (lambda: ap(r).bitcast(dt.uint8)) if codes else (lambda: ap(r)), lambda: src[:], list(after), [r])

    def send(t, k, src, dst, codes=False):
        peer = T.cores[rank ^ (1 << t)]
        rid, pid = topo.addr(peer)[:2]
        n = len(topo.engines(core, peer))
        view = (lambda r: ap(r).bitcast(dt.uint8)) if codes else ap
        sem = "a%d" % (3 * t + k)
        state["glue"] = sem
        op("g", lambda: g.remote_dma(view(dst), view(src), T.sem[sem], T.sem["sent"], pid, rid, topo.mask(core, peer)), [src], [], kind="remote", n=n)
        ops.append({"q": "far", "r": [], "w": [dst], "sem": sem, "n": len(topo.engines(peer, core)), "kind": "far", "glue": sem})
        state["glue"] = None

    def col(name, c):
        return R(name, c, c + 1)

    load("s", "fvi", T.fv)
    load("y", "xs", T.x)
    load("y", "us", T.u)
    p = col("ci", 0)
    iota(p, [[0, 1]], 0, 1)
    iota(R("idb"), [[128, TILES], [1, 16]], 0, 0, False)
    wide = 128 * max(b - a for c in P["rounds"] for a, b in c["ties"])
    fill(R("ones", 0, wide), 1.0)
    op("g", lambda: g.affine_select(ap(R("hole", 0, wide)), ap(R("ones", 0, wide)), [[0, wide // 128], [-1, 128]], A.not_equal, -1.0, 0, 1),
       [R("ones", 0, wide)], [R("hole", 0, wide)])
    fill(R("hole", 0, wide, 128), 0.0)
    iota(R("cnt"), [[1, F]], 0, 0, False)
    fill(R("oz", 0, 8), 0)
    fill(R("oz", 8, 16), 1)
    ts(col("ci", 3), p, 4, A.arith_shift_right, 1, A.bitwise_and)
    ts(col("ci", 4), p, 112, A.bitwise_and)
    ts(col("ci", 5), p, 15, A.bitwise_and)
    copy(R("cf", 0, 2), R("ci", 4, 6))
    tt(col("ci", 6), col("ci", 5), col("ci", 3), A.subtract)
    ts(col("ci", 7), col("ci", 6), 1.0, A.add)
    ts(col("ci", 8), col("ci", 7), 1, A.arith_shift_right)
    ts(col("ci", 9), col("ci", 6), 1, A.bitwise_and)
    ts(col("ci", 10), col("ci", 9), 4.0, A.mult)
    tt(col("ci", 12), col("ci", 10), col("ci", 8), A.add)
    ts(col("off16", 0), col("ci", 12), 7.0, A.min)
    for b in range(4):
        ts(R("l4", 56 * b, 56 * b + 56), R("fvi"), 4.0, A.mult, float(b), A.add)
    load("y", "wq", T.wc, [R("xs")], True)
    load("y", "wsc", T.ws, [R("xs")])
    load("y", "wys", T.wy, [R("xs")])
    ts(R("ids"), R("idb"), col("cf", 0), A.add)

    def gather_h(t, a, e):
        for b in range(4):
            out = R("h%d" % t, 4 * a + b, 4 * e, 4)
            if t == 0:
                scaled(out, (R("xs"), R("l4", 56 * b + a // 16, 56 * b + e // 16)))
            else:
                scaled(out, (R("pl%d" % b, 0, V), R("l1", a // 16, e // 16)), 1.0 / 64)

    def ranks(t):
        c = P["rounds"][t]
        h, qh, sh, ur, sr, pos, cb, win = ("%s%d" % (n, t) for n in ("h", "qh", "sh", "ur", "sr", "pos", "cb", "wa"))
        iota(R(win, 2 * (F - 128), 2 * (F + 16)), [[0, 288]], 0, 0, False)

        def seen(e, a, b):
            lo, bank = [(r[1], r[3]) for r in c["rows"] if r[0] == e and r[1] <= a and b <= r[2]][0]
            return R("ps", 512 * bank + a - lo, 512 * bank + b - lo)

        spans, width = [], []
        for j in range(TILES):
            taken = sorted([c["scalar"][j], (128 * j, 128 * j + 128)])
            runs = []
            for e, a, b, bank in c["rows"]:
                if e == "v":
                    for x, y in taken:
                        if x < b and y > a:
                            if x > a:
                                runs.append((a, x))
                            a = max(a, y)
                    if a < b:
                        runs.append((a, b))
            spans.append(runs)
            width.append(sum(b - a for a, b in runs))
            a, b = c["scalar"][j]
            k = 2 * (F - 65 - (b - a if a < 128 * j else 0))
            iota(R(cb, CB * j + width[j], CB * j + width[j] + 2), [[k % 16 - k // 16 * 16, 2]], k // 16 * 16, 0, False)
        for a, b in c["gather"]:
            gather_h(t, a, b)
        for a, b in c["quant"]:
            quant(R(qh, a, b), R(sh, a, b), R(h, 4 * a, 4 * b))
        for a, b, bank in c["pivots"]:
            for j in range(a, b):
                mx(bank + j - a, 128, R(qh, 128 * j, 128 * j + 128), R(sh, 128 * j, 128 * j + 128), R(ur), R(sr))
            scaled(R(pos, a, b), R("ps", 512 * bank, 512 * (bank + b - a - 1) + 1, 512))
        for e, a, b, bank in c["rows"]:
            mx(bank, b - a, R(ur), R(sr), R(qh, a, b), R(sh, a, b))
        for j in range(TILES):
            own, pv, (a, b) = 128 * j, col(pos, j), c["scalar"][j]
            act(R("sgo", own, own + 128), seen("s", own, own + 128), ACT.Sign, bias=pv, scale=-1.0, accum=col("sa", j))
            act(R("sg", SG * j, SG * j + b - a), seen("s", a, b), ACT.Sign, bias=pv, scale=-1.0)
            act(R("sg2", SG * j, SG * j + b - a), R("sg", SG * j, SG * j + b - a), ACT.Relu, scale=2.0 if a < own else -2.0, accum=col("sb", j))
            at = CB * j
            for a, b in spans[j]:
                ts(R(cb, at, at + b - a), seen("v", a, b), pv, A.is_ge if a < own else A.is_gt, -2.0, A.mult)
                at += b - a
        for a, b in c["ties"]:
            ts(R("eq", 128 * a, 128 * b), R("sgo", 128 * a, 128 * b), 0.0, A.is_equal)
            scan(R("tie", 128 * a, 128 * b), R("hole", 0, 128 * (b - a)), R("eq", 128 * a, 128 * b), 0.0, A.mult, A.add)
        for j in range(TILES):
            at, w, end = CB * j, width[j] // 2 + 1, SC * (j + 1)
            scan(R("sc", end - w, end), R(cb, at, at + w), R(cb, at + w, at + 2 * w), col("tie", 128 * j + 127), A.add, A.add)
            ts(col("ru", j), col("sc", end - 1), col("sa", j), A.add, col("sb", j), A.add if c["scalar"][j][0] < 128 * j else A.subtract)
        for a, b in c["runs"]:
            copy((R(win), R("ru", a, b)), R("ids", 16 * a, 16 * b))

    def fired(t):
        win, lst, at = "wa%d" % t, "lst%d" % t, 2 * (F - K)
        turn(R("tt", 0, 128), R(win, at, at + 256, 2))
        turn(R("tt", 128, 256), R(win, at - 32, at + 224, 2))
        tt(R("q1"), R("tt", 0, 256, 32), R("tt", 16, 256, 32), A.add)
        state["glue"] = lst
        tt(R("q2", p1=64), R("q1", p1=64), R("q1", p0=64), A.add)
        for a in range(4):
            tt(R("q3", p0=32 * a, p1=32 * a + 32), R("q2", p1=32), R("q2", p0=32, p1=64), A.add)
        copy(R(lst), (R("q3"), col("off16", 0)))
        state["glue"] = None
        off = R(lst, 0, TILES)
        send(t, 0, R(lst, 0, 8), R("got%d" % t))
        pick_codes(R("slot%d" % t), R("qh%d" % t), off)
        scaled(R("sls%d" % t), (R("sh%d" % t), off))
        send(t, 1, R("slot%d" % t), R("land%d" % t, 0, K), True)
        send(t, 2, R("sls%d" % t), R("lands%d" % t, 0, K))

    def report(t):
        rev, row = R("frev%d" % t), R("frow%d" % t)
        scaled(rev, (R("cnt"), R("lst%d" % t, 0, TILES)))
        scaled(row, (rev, R("rev", 0, TILES)))
        dma("y", lambda: T.fl[t:t + 1, :], lambda: ap(R(row[0], p1=1)), [row], [])

    def update(t):
        got, ow = R("got%d" % t, 0, TILES), "ow%d" % t
        scaled(R("vrow"), (R("fvt"), got))
        for a, b in P["vm"][t]:
            tt(R("vm", 16 * a, 16 * b), (R("fvt"), R(got[0], a, b)), R("dm", 16 * a, 16 * b), A.mult)
            scan(R("own", 16 * a, 16 * b), R("sm", 16 * a, 16 * b), R("vm", 16 * a, 16 * b), 0.0, A.mult, A.add)
        for b in range(4):
            ts(R(ow, TILES * b, TILES * b + TILES), got, 4.0, A.mult, float(b), A.add)
        for a, b in ((0, 2), (2, 4)):
            scaled(R("x32", K * a, K * b), (R("h%d" % t), R(ow, TILES * a, TILES * b)), 32.0)
        for c in range(TILES):
            mine = col("own", 16 * c + 15)
            ts(R("ev", K * c + 16 * c, K * c + K), R("vrow", 16 * c, K), mine, A.is_equal, mine, A.mult)
        for a, b in P["dd"][t]:
            scan(R("dd", 128 * a, K * b), R("rm", 128 * a, K * b), R("ev", 128 * a, K * b), 0.0, A.mult, A.add)
        ends = R("dd", K - 1, TILES * K, K)
        for b in range(4):
            mx(4 + b, 128, R("wq", 128 * b, 128 * b + 128), R("wsc", 128 * b, 128 * b + 128), R("land%d" % t, 0, 128), R("lands%d" % t, 0, 128))
            tt(R("n64", K * b, K * b + K), R("ps", 512 * (4 + b), 512 * (4 + b) + K), R("x32", K * b, K * b + K), A.add)
        if t == 0:
            off = R("ol0", 0, TILES)
            ts(off, ends, -float(V), A.add)
            for b in range(4):
                copy((R("pl%d" % b), off), R("n64", K * b, K * b + K))
        else:
            for b in range(4):
                scaled(R("nx", K * b, K * b + K), R("n64", K * b, K * b + K), 1.0 / 64)
                ts(R("ol1", TILES * b, TILES * b + TILES), ends, 4.0, A.mult, float(b - 4 * V), A.add)
            copy((R("xi"), R("ol1")), R("nx"))

    quant(R("qu"), R("su"), R("us"))
    pick_codes(R("ur0"), R("qu"), R("oz", 0, 8))
    scaled(R("sr0"), (R("su"), R("oz", 0, 8)))
    ranks(0)
    fired(0)
    copy(R("l1"), R("fvi"))
    scaled(R("fvt", 0, V), (R("cnt", V, F), R("l1", 0, 28)))
    scaled(R("fvt", V, F), (R("cnt", V, F), R("l1", 28, 56)))
    quant(R("land0", K, K + 128), R("lands0", K, K + 128), R("xs", 0, 512))
    for b in range(4):
        scaled(R("pl%d" % b, 0, V), R("xs", b, 4 * V, 4), 64.0)
    pick_codes(R("ur1"), R("qu"), R("oz", 8, 16))
    scaled(R("sr1"), (R("su"), R("oz", 8, 16)))
    iota(R("sm"), [[0, TILES], [1, 16]], 0, 0, False)
    iota(R("rvi"), [[-16, 8]], K - 1, 0)
    ts(R("dm"), R("sm"), col("cf", 1), A.is_equal)
    ts(R("sm"), R("sm"), 0.0, A.not_equal)
    ts(R("rm", 0, 128), R("cnt", 0, 128), col("cf", 1), A.not_equal)
    for a, b in ((128, 256), (256, 512), (512, F)):
        copy(R("rm", a, b), R("rm", 0, b - a))
    ts(R("ev"), R("rm", 0, TILES * K), 0.0, A.mult)
    ts(R("rev"), R("rvi"), col("cf", 1), A.subtract)
    update(0)

    ranks(1)
    fired(1)
    quant(R("land1", K, K + 128), R("lands1", K, K + 128), R("xs", 0, 512))
    for b in range(4):
        scaled(R("xi", b, 4 * V, 4), R("pl%d" % b, 0, V), 1.0 / 64)
    report(0)
    report(1)
    quant(R("qwy"), R("swy"), R("wys"))
    update(1)

    a = 0
    for half, n in enumerate(P["out"]):
        b = a + n
        q, s, y = R("qx", a, b), R("sx", a, b), R("ysb", a, b)
        quant(q, s, R("xi", 4 * a, 4 * b))
        mx(half, n, R("qwy"), R("swy"), q, s)
        dma("y", lambda a=a, b=b: T.oc[:, 4 * a:4 * b], lambda q=q: ap(q).bitcast(dt.uint8), [q], [])
        scaled(y, R("ps", 512 * half, 512 * half + n))
        dma("sy"[half % 2], lambda a=a, b=b: T.y[:, a:b], lambda y=y: ap(y), [y], [])
        a = b
    for k in range(4):
        s = R("sx", p0=32 * k, p1=32 * k + 4)
        dma("ys"[k % 2], lambda k=k: T.osc[4 * k:4 * k + 4, :], lambda s=s: ap(s), [s], [])
    return ops


def rank_program(g, core, T, topo):
    rank = T.rank_of(core)
    if rank is not None:
        _emit(g, T, _order(_record(g, core, T, topo, rank)))
